import numpy as np, ml_dtypes
CORES = [30,158,46,174,86,214]
N = 6
BF = ml_dtypes.bfloat16
W, L, M, P, Q, F, RO = 2048, 16, 6, 32, 16, 6, 2
CAP = (N - 1) * Q
def look(u, m):
    return (u * (u >> 5) + (2 * m + 1) * u) & (W - 1)
def pick(x, ix):
    return np.take_along_axis(x, ix[..., None, :], -1)
def pack(x, w, th):
    return {"x0": np.ascontiguousarray(x.reshape(N, 128, W)).astype(np.float32).astype(BF), "wt": np.ascontiguousarray(w).reshape(N, 128, 1).astype(np.float32).astype(BF),
            "th": np.repeat(th, 16, axis=1).astype(np.int32)}
def texture(rng):
    x = np.empty((N, 8, 16, W), np.int64); stock = rng.permutation(np.array([8, 24, 60, 120, 200, 300, 400, 600]))
    for g in range(8):
        n = int(stock[g]); base = rng.integers(0, 256, (n, 16))
        for q in range(N):
            e = 1.5 + rng.random()
            x[q, g] = (base[np.minimum((n * rng.random(W) ** e).astype(np.int64), n - 1)] + rng.integers(-2, 3, (W, 16))).T
    return np.clip(x, 0, 255)
def far(rng):
    return rng.integers(0, 256, (N, 8, 16, W))
def weights(rng):
    w = rng.integers(0, 256, (8, 16)); w[:, 0] = 1; w[:, 1] = 16; w[:, 13:] = 0
    return w
def with_hash(rng, w, u):
    k = rng.integers(0, 256, (len(u), 16)); v = (u - k[:, 2:] @ w[2:]) & (W - 1)
    k[:, 0] = v & 15; k[:, 1] = v >> 4
    return k
def odd(rng, m, n):
    u = np.arange(1, W, 2); u = rng.permutation(u[((u >> 5) & 1) == 0])
    i = np.unique(look(u, m), return_index=True)[1]
    assert len(i) >= n
    return rng.permutation(u[i])[:n]
def runs(rng):
    r = W // (L + F); n = min(r, CAP + 12)
    return L * np.sort(rng.permutation(r)[:n]) + L - 2
def setup_inputs(rng):
    return pack(texture(rng), rng.integers(0, 256, (N, 8, 16)), rng.integers(20, 41, (N, 8, 2)))
def setup_inputs_room(rng):
    x = far(rng); w = weights(rng); th = np.stack([rng.integers(1, 60, (N, 8)), rng.choice(np.array([1, 2, 40]), (N, 8))], axis=-1)
    th[rng.integers(0, N), rng.integers(4, 6), 1] = 0
    for g in range(8):
        m = g % M; p = runs(rng); n = len(p); u = odd(rng, m, n); c = look(u, m); k = with_hash(rng, w[g], u)
        for q in range(N):
            a = int(rng.choice(np.array([0, 1, CAP - 1, CAP, CAP + 1, n])))
            if q == 0: a = (CAP, CAP + 1, n, CAP - 1, 1, 0, CAP, CAP + 1)[g]
            i = rng.permutation(n)[:a]
            x[q, g][:, c] = k.T; x[q, g][:, p[i]] = k[i].T
    return pack(x, np.broadcast_to(w, (N, 8, 16)), th)
def setup_inputs_ties(rng):
    x = far(rng); w = weights(rng); t = rng.integers(2, 250, 8); t2 = t + rng.integers(-1, 2, (N, 8))
    for g in range(1, 8, 2):
        a = 4 * int(rng.integers(65, 124)) + g % 4; t2[:, g] = a; t[g] = a + int(rng.integers(0, 2))
    th = np.stack([np.broadcast_to(t, (N, 8)), t2], axis=-1)
    for g in range(8):
        m = g % M; p = runs(rng); n = len(p); u = odd(rng, m, n); k = with_hash(rng, w[g], u); k[:, 13:] = 0; more = 255 * (g % 2)
        for q in range(N):
            for c in (look(u, m + 1), look(u, m)):
                z = k + 0; z[:, 14] = rng.integers(0, 3, n); x[q, g][:, c] = z.T
            z = k + 0; z[:, 13] = more; z[:, 15] = t[g] - more + rng.integers(-2, 1, n); x[q, g][:, p] = z.T
    return pack(x, np.broadcast_to(w, (N, 8, 16)), th)
def over_the_end(rng, x, w, g):
    p = W - L - 2; every = np.arange(W); first = look(every, 0); later = look(every, np.arange(1, P)[:, None])
    good = (first >= L) & (first < p - L)
    j, uk = np.nonzero((later > W - F) & good & ~np.any(later == p, axis=0))
    i = int(rng.integers(0, len(uk))); u = int(uk[i]); c1 = int(first[u]); c2 = int(later[j[i], u])
    a = int(rng.choice(every[good & (first != c1)])); ca = int(first[a])
    k = with_hash(rng, w[g], np.array([u]))[0]; k[15] = 0; near = k + 0; near[15] = 3
    ka = with_hash(rng, w[g], np.full(N, a))
    for q in range(N):
        x[q, g][:, [0, ca]] = ka[q][:, None]; x[q, g][:, c1] = near; x[q, g][:, [p, c2 - F]] = k[:, None]
def setup_inputs_ends(rng):
    x = far(rng); w = weights(rng); th = rng.integers(1, 60, (N, 8, 2))
    mm, uu = np.nonzero(look(np.arange(W), np.arange(M)[:, None]) >= W - L // 2)
    for g in range(8):
        if g % 4 == 3:
            over_the_end(rng, x, w, g); th[:, g] = rng.integers(4, 60, (N, 2))
            continue
        if g % 2 == 0:
            o = rng.permutation(len(uu)); c, i = np.unique(look(uu[o], mm[o]), return_index=True); u = uu[o][i]; p = L * rng.permutation(len(u))
        else:
            u = odd(rng, g % M, 1); c = look(u, g % M); p = np.array([W - 2])
        k = with_hash(rng, w[g], u)
        for q in range(N):
            x[q, g][:, c] = k.T; x[q, g][:, p] = k.T
    return pack(x, np.broadcast_to(w, (N, 8, 16)), th)
def setup_inputs_alike(rng):
    x = texture(rng); w = rng.integers(0, 256, (N, 8, 16)); th = rng.integers(20, 41, (N, 8, 2))
    for g in range(0, 8, 2):
        base = rng.integers(0, 256, (4, 16)); x[:, g] = base[rng.integers(0, 4, (N, W))].transpose(0, 2, 1)
    th[:, 0] = 1; th[:, 2] = 4096; th[:, 4, 0] = 0; th[:, 1, 0] = 4096; th[:, 1, 1] = 0; th[:, 3, 1] = 4096
    w[:, 6] = 0; w[:, 5] = 255
    x[:, 1, :, 0] = 255
    w[:, 7] = rng.integers(230, 256, (N, 16))
    up = rng.random((N, 1, W)) < 0.5; up[::2] = False
    x[:, 7] = np.where(up, 255 - rng.integers(0, 40, (N, 16, W)), rng.integers(0, 40, (N, 16, W)))
    for q in range(N):
        x[q, 1][:, L * (1 + rng.permutation(W // L - 1)[:W // L // 2])] = 0
        if q % 2 == 0:
            th[q, 7, 0] = rng.integers(150, 260); th[q, 7, 1] = rng.integers(3100, 3600)
        else:
            th[q, 7, 0] = rng.integers(2048, 3000); th[q, 7, 1] = rng.integers(100, 4097)
            c = look((255 * int(np.sum(w[q, 7]))) & (W - 1), 0); x[q, 7][:, [0, L, c]] = 255
    th[0, 7, 1] = 4096
    return pack(x, w, th)
def setup_inputs_spread(rng):
    x = np.minimum((np.exp2(8 * rng.random((N, 8, 1, W))) * rng.random((N, 8, 16, W))).astype(np.int64), 255)
    w = np.minimum(np.exp2(8 * rng.random((N, 8, 16))).astype(np.int64), 255) * (rng.random((N, 8, 16)) > 0.0625)
    return pack(x, w, np.minimum(np.exp2(12 * rng.random((N, 8, 2))).astype(np.int64), 4096))
def check_inputs(d):
    bad = []
    for k in ("x0", "wt"):
        v = np.asarray(d[k]).astype(np.float32)
        if not np.all((v >= 0) & (v <= 255) & (v == np.floor(v))): bad.append("whole numbers of " + k)
    v = np.asarray(d["th"])
    if np.min(v) < 0 or np.max(v) > 4096: bad.append("range of th")
    v = v.reshape(N, 8, 16, 2)
    if np.any(v != v[:, :, :1]): bad.append("rows of th alike in a group")
    return bad
def reference(x0, wt, th):
    x = x0.astype(np.float32).astype(np.int64).reshape(N, 8, 16, W); w = wt.astype(np.float32).astype(np.int64).reshape(N, 8, 16, 1)
    t = th.astype(np.int64).reshape(N, 8, 16, 2)[:, :, 0]; here = np.arange(W)
    for rnd in range(RO):
        u = np.add.reduce(w * x, axis=2) & (W - 1)
        nx = np.zeros_like(u) + ((here + 1) & (W - 1))
        for m in range(M - 1, -1, -1):
            c = look(u, m); near = np.add.reduce(np.abs(pick(x, c) - x), axis=2) < t[..., :1]
            nx = np.where(near, (c + 1) & (W - 1), nx)
        s = np.zeros((N, 8, W // L, L), np.int64); s[..., 0] = L * np.arange(W // L)
        for k in range(1, L): s[..., k] = np.take_along_axis(nx, s[..., k - 1], -1)
        jump = np.zeros(s.shape, bool); jump[..., :-1] = s[..., 1:] != ((s[..., :-1] + 1) & (W - 1))
        s = s.reshape(N, 8, W); jump = jump.reshape(N, 8, W)
        site = np.argsort(~jump, axis=-1, kind="stable")[..., :CAP]
        live = np.take_along_axis(jump, site, -1); ask = pick(x, np.take_along_axis(s, site, -1))
        found = np.zeros((N, 8, CAP), bool); fill = np.zeros((N, 8, 16, CAP, F), np.int64)
        for q in range(N):
            for d in range(1, N):
                b = (q + d) % N; cut = slice((d - 1) * Q, d * Q); a = ask[q][:, :, cut]
                v = np.add.reduce(w[b] * a, axis=1) & (W - 1); c = look(v[..., None], np.arange(P))
                off = np.add.reduce(np.abs(pick(x[b], c.reshape(8, -1)).reshape(8, 16, Q, P) - a[..., None]), axis=1)
                best = np.take_along_axis(c, np.argmin(off, axis=-1)[..., None], -1)
                found[q][:, cut] = np.min(off, axis=-1) < t[b][:, 1:]
                fill[q][:, :, cut] = pick(x[b], ((best + 1 + np.arange(F)) & (W - 1)).reshape(8, -1)).reshape(8, 16, Q, F)
        found = found & live
        more = np.zeros((N, 8, W), np.int64); np.put_along_axis(more, site, found.astype(np.int64) * F, -1)
        place = here + np.add.accumulate(more, axis=-1) - more
        z = np.zeros((N, 8, 16, W + F * CAP + 1), np.int64)
        np.put_along_axis(z, place[:, :, None], pick(x, s), -1)
        at = np.take_along_axis(place, site, -1)[..., None] + 1 + np.arange(F)
        at = np.where(found[..., None], at, W + F * CAP).reshape(N, 8, 1, CAP * F)
        np.put_along_axis(z, at, fill.reshape(N, 8, 16, CAP * F), -1)
        x = np.ascontiguousarray(z[..., :W])
    return {"y": x.reshape(N, 128, W).astype(np.float32).astype(BF)}

@@ -1,0 +1,578 @@
+import numpy as np
+from concourse.bass import DstId, RemoteDMATransfer
+from concourse.mybir import dt, AluOpType as Op, AxisListType, ActivationFunctionType as Fn
+
+N, W, L, M, P, Q, F, RO = 6, 2048, 16, 6, 32, 16, 6, 2
+H = W // 2
+HJ = H // 16
+ND = N - 1
+SLOT = Q * F + 8
+RING = 6
+XW = 3072
+
+SB = {}
+PART = {}
+ARENA = {"int32": ["ar_i", 0], "float32": ["ar_f", 0], "bfloat16": ["ar_b", 0], "uint16": ["ar_u", 0]}
+OWN = ("WT", "TH")
+
+
+def sb(name, cols, dtype):
+    if cols <= 160 and dtype in ARENA and name not in OWN and not name.startswith(("QIN", "ASK")):
+        a = ARENA[dtype]
+        PART[name] = (a[0], a[1], cols)
+        a[1] += -(-cols // 16) * 16
+    else:
+        SB[name] = ("sbuf", [128, cols], dtype)
+
+
+def many(names, cols, dtype):
+    for n in names.split():
+        sb(n, cols, dtype)
+
+
+many("XA XB XC", XW, "bfloat16")
+many("XP Xst Xnat WEI EI", W, "bfloat16")
+sb("BIh", W, "float16")
+many("D AB", RING * H, "bfloat16")
+sb("G", 2 * H, "bfloat16")
+many("i_ui i_ua i_us i_u2 i_r1 i_r2 i_nxw", 2 * HJ, "int32")
+many("raw msk", 2 * M * HJ, "int32")
+sb("lst", 2 * M * HJ, "uint16")
+sb("RUN", 2 * M * HJ, "float32")
+sb("RG", 2 * M * HJ, "bfloat16")
+many("f_r f_d f_e", 2 * HJ, "float32")
+sb("NXH", 2 * HJ, "float16")
+sb("NXW", W, "float32")
+many("CM CS", 256, "float32")
+many("LC LF PL", 128, "uint16")
+many("SW J", 128, "float32")
+many("dif dif2", 128, "int32")
+many("INC ING DEL", 128, "bfloat16")
+many("GO CC EQ LT LO", 640, "bfloat16")
+sb("AL", 8, "uint16")
+many("plc live pl8", 8, "float32")
+for _r in range(RO):
+    many("ASK%d QIN%d" % (_r, _r), ND * Q, "bfloat16")
+    many("FIL%d ZIN%d" % (_r, _r), ND * SLOT, "bfloat16")
+sb("QREP", 12 * ND * Q, "bfloat16")
+many("VM VS", 80, "float32")
+many("q_vi q_va q_vs q_vb q_ki q_km q_kc q_kd", 8, "int32")
+many("q_c0 q_v2 q_KM q_kt", 8, "float32")
+many("qraw qmsk", P * ND, "int32")
+sb("qlst", P * ND, "uint16")
+many("FL SLu", 32, "uint16")
+sb("an", 8, "bfloat16")
+sb("a8", 8, "int32")
+sb("ahl", 16, "int32")
+sb("ahf", 16, "float32")
+many("SL SL2", 32, "float32")
+many("ONB WBLK", 128, "bfloat16")
+many("k_TMP k_BLK k_IDN k_LST1 k_LST6 k_BLK6 k_NB6 k_SHF k_DSH k_ID16 k_NEGI k_N8I k_JJ k_IP1 k_IARRt k_IARR k_ICOL", 128, "bfloat16")
+many("k_NP1 k_NARRt k_NARR", 640, "bfloat16")
+sb("k_MROWf", P * ND, "float32")
+sb("k_MROW", P * ND, "bfloat16")
+sb("k_MC", P, "float32")
+many("k_MKi k_MKa", 128, "int32")
+many("k_MK k_RS k_ONF k_PWb k_PW1", 128, "float32")
+sb("k_RB5", (M - 1) * HJ, "float32")
+many("k_p k_p2 TH", 8, "int32")
+many("k_I16 k_I64 k_I128 k_LB k_T", 8, "float32")
+sb("k_L0", 8, "uint16")
+many("k_CW k_GW WT", 8, "bfloat16")
+many("k_JKb k_JK", 32, "float32")
+for _k in range(8):
+    SB["ps%d" % _k] = ("psum", [128, 512], "float32")
+for _d in ARENA:
+    SB[ARENA[_d][0]] = ("sbuf", [128, ARENA[_d][1]], _d)
+SCRATCH = SB
+SEMAPHORES = ["sV", "sS", "sT", "sG", "lsem", "dx0", "dx1", "dwt", "dth", "dy0", "dy1", "q0", "q1", "z0", "z1"]
+
+WB = ((2, 7), (4, 5))
+PLAN = [tuple(int(c) if c.isdigit() else c for c in x.split(".")) for x in (
+    "v.0.0 v.0.2 lists v.0.3 sg.0.4 sub.0.4 v.1.2 v.1.1 a.0.0 a.0.2 sl.0.4 v.0.1 sg.1.4 sub.1.4 a.1.2 a.1.1 a.0.3 v.1.0 v.1.3 consts "
+    "a.0.1 sl.1.4 a.1.0 a.1.3 v.0.5 first.0 v.1.5 a.0.5 first.1 bl.0 a.1.5 succ.0 bl.1 succ.1 win.0 win.1").split()]
+
+
+def rank_program(g, core, T, topo):
+    rank = T.rank_of(core)
+    if rank is None:
+        return
+    cores = T.cores
+    queue = {"V": g.vector, "S": g.scalar, "T": g.tensor, "G": g, "Y": g.sync}
+    semof = {"V": "sV", "S": "sS", "T": "sT", "G": "sG"}
+    cnt = {"V": 0, "S": 0, "T": 0, "G": 0}
+    known = {"V": {}, "S": {}, "T": {}, "G": {}, "Y": {}}
+    snap = {}
+    log = {}
+
+    def A(name, c0=0, c1=None, step=1):
+        if name in PART:
+            a, o, n = PART[name]
+            return (a, o + c0, o + (n if c1 is None else c1), step)
+        n = SB[name][1][1]
+        return (name, c0, n if c1 is None else c1, step)
+
+    def ap(a):
+        return T[a[0]][:, a[1]:a[2]:a[3]] if a[3] != 1 else T[a[0]][:, a[1]:a[2]]
+
+    def overlap(a, b):
+        if a[1] >= b[2] or b[1] >= a[2]:
+            return False
+        if a[3] == b[3] and a[3] > 1 and (a[1] - b[1]) % a[3]:
+            return False
+        return True
+
+    def wait(e, sem, val):
+        k = known[e]
+        if k.get(sem, 0) >= val:
+            return
+        queue[e].wait_ge(T.sem[sem], val)
+        s = snap.get((sem, val))
+        if s:
+            for q in s:
+                if s[q] > k.get(q, 0):
+                    k[q] = s[q]
+        k[sem] = val
+
+    def need(e, reads, writes):
+        own = semof.get(e)
+        req = {}
+        for lst, isw in ((reads, False), (writes, True)):
+            for a in lst:
+                ps = SB[a[0]][0] == "psum"
+                for (w, b, sem, val) in log.get(a[0], ()):
+                    if sem == own:
+                        if not w or (ps and e == "T" and isw) or not overlap(a, b):
+                            continue
+                    elif not ps:
+                        if not (w or isw) or not overlap(a, b):
+                            continue
+                    if val > req.get(sem, 0):
+                        req[sem] = val
+        for s in sorted(req, key=lambda s: -req[s]):
+            wait(e, s, req[s])
+
+    def covers(a, b):
+        return a[1] <= b[1] and a[2] >= b[2] and (a[3] == 1 or (a[3] == b[3] and (a[1] - b[1]) % a[3] == 0))
+
+    def note(reads, writes, sem, val):
+        for a in writes:
+            l = log.get(a[0], [])
+            if SB[a[0]][0] != "psum":
+                l = [x for x in l if not covers(a, x[1])]
+            else:
+                l = [x for x in l if not (x[0] and x[2] == sem and covers(a, x[1]))]
+            l.append((True, a, sem, val))
+            log[a[0]] = l
+        for a in reads:
+            l = log.setdefault(a[0], [])
+            l[:] = [x for x in l if x[0] or x[2] != sem or not covers(a, x[1])]
+            l.append((False, a, sem, val))
+
+    def do(e, fn, reads, writes):
+        need(e, reads, writes)
+        cnt[e] += 1
+        fn().then_inc(T.sem[semof[e]], 1)
+        snap[(semof[e], cnt[e])] = dict(known[e])
+        note(reads, writes, semof[e], cnt[e])
+
+    def dma(e, out, in_, sem, reads, writes):
+        need(e, reads, writes)
+        queue[e].dma_start(out=out, in_=in_).then_inc(T.sem[sem], 16)
+        snap[(sem, 16)] = dict(known[e])
+        note(reads, writes, sem, 16)
+
+    def is_ap(x):
+        return isinstance(x, tuple)
+
+    def val(x):
+        return ap(x) if is_ap(x) else x
+
+    def cp(out, in_):
+        do("V", lambda: g.vector.tensor_copy(ap(out), ap(in_)), [in_], [out])
+
+    def tt(out, a, b, op):
+        do("V", lambda: g.vector.tensor_tensor(ap(out), ap(a), ap(b), op), [a, b], [out])
+
+    def ts(out, a, s1, op0, s2=None, op1=None):
+        rd = [a] + [s for s in (s1, s2) if is_ap(s)]
+        if op1 is None:
+            do("V", lambda: g.vector.tensor_scalar(ap(out), ap(a), val(s1), None, op0), rd, [out])
+        else:
+            do("V", lambda: g.vector.tensor_scalar(ap(out), ap(a), val(s1), val(s2), op0, op1), rd, [out])
+
+    def ms(out, c):
+        do("V", lambda: g.vector.memset(ap(out), c), [], [out])
+
+    def scan(out, d0, d1, op0, op1):
+        do("V", lambda: g.vector.tensor_tensor_scan(ap(out), ap(d0), ap(d1), 0.0, op0, op1), [d0, d1], [out])
+
+    def act(out, in_, func=Fn.Copy, scale=1.0):
+        do("S", lambda: g.scalar.activation(ap(out), ap(in_), func, scale=val(scale)), [in_] + ([scale] if is_ap(scale) else []), [out])
+
+    def mm(out, l, r, start, stop):
+        do("T", lambda: g.tensor.matmul(ap(out), ap(l), ap(r), start, stop), [l, r], [out])
+
+    def vgather(out, win, off, b=None, op=None):
+        if b is None:
+            do("V", lambda: g.vector.tensor_copy(ap(out), ap(win).indirect(ap(off))), [win, off], [out])
+        else:
+            do("V", lambda: g.vector.tensor_tensor(ap(out), ap(win).indirect(ap(off)), ap(b), op), [win, off, b], [out])
+
+    def sgather(out, win, off):
+        do("S", lambda: g.scalar.activation(ap(out), ap(win).indirect(ap(off)), Fn.Copy), [win, off], [out])
+
+    def scatter(win, off, in_):
+        do("V", lambda: g.vector.tensor_copy(ap(win).indirect(ap(off)), ap(in_)), [off, in_], [win])
+
+    def iota(out, pattern, base, chan, flag=False):
+        if flag:
+            do("G", lambda: g.iota(ap(out), pattern, base, chan, allow_small_or_imprecise_dtypes=True), [], [out])
+        else:
+            do("G", lambda: g.iota(ap(out), pattern, base, chan), [], [out])
+
+    def asel(out, in_, pattern, op, base, chan):
+        do("G", lambda: g.affine_select(ap(out), ap(in_), pattern, op, 0.0, base, chan), [in_], [out])
+
+    dma("Y", T.WT[:, 0:1], T.wt[:, :], "dwt", [], [A("WT", 0, 1)])
+    dma("Y", T.XA[:, 0:H], T.x0[:, 0:H], "dx0", [], [A("XA", 0, H)])
+    dma("S", T.XA[:, H:W], T.x0[:, H:W], "dx1", [], [A("XA", H, W)])
+    dma("S", T.TH[:, 0:2], T.th[:, :], "dth", [], [A("TH", 0, 2)])
+
+    K = lambda n, c0=0, c1=None, step=1: A("k_" + n, c0, c1, step)
+    ms(A("ONB"), 1.0)
+    asel(K("TMP"), A("ONB"), [[-16, 8], [0, 16]], Op.is_ge, 0, 1)
+    asel(K("BLK"), K("TMP"), [[16, 8], [0, 16]], Op.is_ge, 15, -1)
+    iota(K("p", 0, 1), [[0, 1]], 0, 1)
+    iota(K("MKi"), [[-1, 128]], 128, 1)
+    iota(K("PWb"), [[H, 2], [1, HJ]], 1, 0, True)
+    iota(K("LB"), [[16, 8]], 0, 0, True)
+    ms(A("WEI"), 0.0)
+    for i in range(16):
+        ts(A("WEI", 128 * i + i, 128 * i + 128, 16), K("BLK", i, 128, 16), A("WT", 0, 1), Op.mult)
+    ms(A("EI"), 0.0)
+    for i in range(16):
+        act(A("EI", 128 * i + i, 128 * i + 128, 16), K("BLK", i, 128, 16))
+    ts(K("p2", 0, 1), K("p", 0, 1), 15, Op.bitwise_and)
+    cp(K("I16", 0, 1), K("p2", 0, 1))
+    ts(K("I64", 0, 1), K("I16", 0, 1), float(HJ), Op.mult)
+    ts(K("I128", 0, 1), K("I16", 0, 1), 128.0, Op.mult)
+    ts(K("PW1"), K("PWb"), K("I64", 0, 1), Op.add)
+    ts(K("L0"), K("LB"), K("I128", 0, 1), Op.add)
+    ts(K("MKa"), K("MKi"), 15, Op.bitwise_and)
+    ts(K("MK"), K("MKa"), 0, Op.is_equal)
+    asel(K("IDN"), A("ONB"), [[-1, 128]], Op.is_equal, 0, 1)
+    ts(K("NEGI"), K("IDN"), -1.0, Op.mult)
+    for i in range(16):
+        ts(A("BIh", 128 * i, 128 * i + 128), K("BLK"), K("MK", i, i + 1), Op.mult)
+    ms(K("RB5"), 0.0)
+    ms(K("RB5", 0, None, M - 1), 100000.0)
+    cp(K("T", 0, 2), A("TH", 0, 2))
+    ms(K("RS"), 1.0)
+    ms(K("RS", 0, None, 16), 0.0)
+    iota(K("NP1"), [[16, ND], [0, 8], [1, 16]], 1, 0, True)
+    iota(K("JJ"), [[1, 128]], 0, 0, True)
+    iota(K("IP1"), [[0, 8], [1, 16]], 1, 0, True)
+    iota(K("MC"), [[1, P]], 0, 0, True)
+    iota(K("MROWf"), [[1, P], [0, ND]], 0, 0, True)
+    iota(K("JKb", 0, 30), [[16, 30]], 2560, 0, True)
+    asel(K("LST1"), K("BLK"), [[1, 128]], Op.is_ge, -1, -1)
+    asel(K("SHF"), K("BLK"), [[1, 128]], Op.is_equal, -1, -1)
+    asel(K("NARRt"), K("NP1"), [[0, ND], [-16, 8], [0, 16]], Op.is_ge, 0, 1)
+    asel(K("NARR"), K("NARRt"), [[0, ND], [16, 8], [0, 16]], Op.is_ge, 15, -1)
+    asel(K("IARRt"), K("IP1"), [[-16, 8], [0, 16]], Op.is_ge, 0, 1)
+    asel(K("IARR"), K("IARRt"), [[16, 8], [0, 16]], Op.is_ge, 15, -1)
+
+    def consts_b():
+        act(K("MROW"), K("MROWf"), scale=1.0 / P)
+        act(K("LST6"), K("LST1"), scale=6.0)
+        act(K("BLK6"), K("BLK"), scale=6.0)
+        act(K("NB6"), K("BLK"), scale=-6.0)
+        act(K("ID16"), K("IDN"), scale=16.0)
+        act(K("N8I"), K("IDN"), scale=-8192.0)
+        act(K("ICOL"), A("ONB"), scale=K("I16", 0, 1))
+        for r in range(RO):
+            act(A("FIL%d" % r), K("NARR", 0, ND * SLOT), scale=0.0)
+
+    def consts_c():
+        ms(K("ONF"), 1.0)
+        tt(K("DSH"), K("IDN"), K("SHF"), Op.subtract)
+        ms(K("CW", 0, 1), 16.0)
+        ms(K("CW", 1, 2), 1.0)
+        ms(K("GW", 0, 1), 1.0)
+        ms(K("GW", 1, 2), 128.0)
+        ts(A("WBLK"), K("BLK"), A("WT", 0, 1), Op.mult)
+        ts(K("JK", 0, 30), K("JKb", 0, 30), K("I16", 0, 1), Op.add)
+
+    def send(src, dst, dest, sem):
+        trs = []
+        for k in range(ND):
+            need("G", [src[k]], [])
+        for k in range(ND):
+            rid, pid = topo.addr(dest[k], core)
+            es = topo.engines(core, dest[k])
+            if k < 4:
+                n = len(es) // 4
+                mask = sum(1 << e for e in es[n * k:n * k + n])
+                trs.append(RemoteDMATransfer(dst_ids=[DstId(rid=rid, pnc=pid)], dma_engine_mask=mask, remote_sem=T.sem[sem],
+                                             src=ap(src[k]), dst=ap(dst[k])))
+                tot[0] += n
+        g.remote_dma_fused(trs, local_sem=T.sem.lsem)
+        g.remote_dma(ap(dst[4]), ap(src[4]), T.sem[sem], T.sem.lsem, pid, rid, topo.mask(core, dest[4]))
+        tot[0] += len(es)
+        return 4 * n + len(es)
+
+    tot, ring, gs, landed, place = [0], [0], [0], {}, {}
+    xs = ("XA", "XB", "XC")
+    ps = lambda k, c0, c1, step=1: A("ps%d" % k, c0, c1, step)
+    for r in range(RO):
+        X, XN = xs[r], xs[r + 1]
+
+        for h in range(2):
+            for i in range(16):
+                mm(ps(h, 0, HJ), A("WEI", 128 * i, 128 * i + 128), A(X, H * h + HJ * i, H * h + HJ * i + HJ), i == 0, i == 15)
+            for i in range(16):
+                act(A("XP", H * h + i, H * h + H, 16), A(X, H * h + HJ * i, H * h + HJ * i + HJ))
+        if r == 0:
+            act(A(X, W, W + 8), A(X, 0, 8))
+
+        def lists(h):
+            o, e = HJ * h, HJ * h + HJ
+            ui, ua, us = [A("i_" + n, o, e) for n in ("ui", "ua", "us")]
+            u2, bb = ps(6, 128, 128 + HJ), ps(6, 256, 256 + HJ)
+            R = lambda m: A("raw", M * HJ * h + HJ * m, M * HJ * h + HJ * m + HJ)
+            al = lambda n: A(n, M * HJ * h, M * HJ * h + M * HJ)
+            cp(ui, ps(h, 0, HJ))
+            ts(ua, ui, W - 1, Op.bitwise_and)
+            ts(us, ui, W - 1, Op.bitwise_and, 5, Op.arith_shift_right)
+            ts(u2, ua, 2, Op.mult)
+            ts(A("i_u2", o, e), ua, 2, Op.mult)
+            tt(bb, ua, us, Op.mult)
+            tt(R(0), bb, ua, Op.add)
+            for m in range(1, M):
+                tt(R(m), u2, R(m - 1), Op.add)
+            ts(al("msk"), al("raw"), W - 1, Op.bitwise_and)
+            cp(al("lst"), al("msk"))
+            ts(A("i_r1", o, e), R(0), 1, Op.add)
+
+        def lk(h, m):
+            return A("lst", M * HJ * h + HJ * m, M * HJ * h + HJ * m + HJ)
+
+        def slot():
+            ring[0] += 1
+            o = H * (ring[0] % RING)
+            return A("D", o, o + H), A("AB", o, o + H), o
+
+        def dist(h, m, o):
+            out = ps(2 + h, m, (M - 1) * HJ, M - 1) if m < M - 1 else ps(h, 0, HJ)
+            for i in range(16):
+                mm(out, A("EI", 128 * i, 128 * i + 128), A("AB", o + i, o + H, 16), i == 0, i == 15)
+
+        def sgath(h, m):
+            gs[0] ^= 1
+            o = H * gs[0]
+            sgather(A("G", o, o + H), A(X, 0, W), lk(h, m))
+            place["g", h, m] = o
+
+        def sub(h, m):
+            o = place["g", h, m]
+            for c in range(2):
+                mm(ps(4 + c, 0, 512), K("IDN"), A("G", o + 512 * c, o + 512 * c + 512), True, False)
+                mm(ps(4 + c, 0, 512), K("NEGI"), A("XP", H * h + 512 * c, H * h + 512 * c + 512), False, True)
+
+        def slook(h, m):
+            d, a, o = slot()
+            for c in range(2):
+                act(A("AB", o + 512 * c, o + 512 * c + 512), ps(4 + c, 0, 512), Fn.Abs)
+            dist(h, m, o)
+
+        def vlook(h, m):
+            d, a, o = slot()
+            place[h, m] = d, a, o
+            vgather(d, A(X, 0, W), lk(h, m), A("XP", H * h, H * h + H), Op.subtract)
+
+        def size(h, m):
+            d, a, o = place[h, m]
+            act(a, d, Fn.Abs)
+            dist(h, m, o)
+
+        def first(h):
+            o, n, s, e = M * HJ * h, (M - 1) * HJ, HJ * h, HJ * h + HJ
+            scan(A("RUN", o, o + n), K("RB5"), ps(2 + h, 0, n), Op.add, Op.min)
+            ts(A("RG", o, o + n), A("RUN", o, o + n), K("T", 0, 1), Op.is_ge)
+            for m in range(M - 1):
+                mm(ps(6, s, e), K("IDN"), A("RG", o + m, o + n, M - 1), m == 0, m == M - 2)
+
+        def before_last(h):
+            o, n, s, e = M * HJ * h, (M - 1) * HJ, HJ * h, HJ * h + HJ
+            ft, fd = ps(6, 128 + s, 128 + e), ps(6, 256 + s, 256 + e)
+            tt(ft, ps(6, s, e), A("i_u2", s, e), Op.mult)
+            tt(A("f_r", s, e), ft, A("i_r1", s, e), Op.add)
+            tt(fd, K("PW1", s, e), A("f_r", s, e), Op.subtract)
+            tt(A("f_e", s, e), fd, A("RG", o + M - 2, o + n, M - 1), Op.mult)
+
+        def succ(h):
+            s, e = HJ * h, HJ * h + HJ
+            ft = ps(6, 128 + s, 128 + e)
+            ts(ft, ps(h, 0, HJ), K("T", 0, 1), Op.is_ge)
+            tt(A("f_d", s, e), ft, A("f_e", s, e), Op.mult)
+            tt(A("i_r2", s, e), A("f_r", s, e), A("f_d", s, e), Op.add)
+            ts(A("i_nxw", s, e), A("i_r2", s, e), W - 1, Op.bitwise_and)
+            cp(A("NXH", s, e), A("i_nxw", s, e))
+            for i in range(16):
+                mm(ps(WB[h][i // 8], HJ * (i % 8), HJ * (i % 8) + HJ), A("BIh", 128 * i, 128 * i + 128), A("NXH", s, e), True, True)
+
+        def window(h):
+            act(A("NXW", H * h, H * h + 512), ps(WB[h][0], 0, 512))
+            cp(A("NXW", H * h + 512, H * h + H), ps(WB[h][1], 0, 512))
+
+        calls = {"sg": sgath, "sub": sub, "sl": slook, "v": vlook, "a": size, "first": first, "bl": before_last, "succ": succ,
+                 "win": window, "lists": lambda: lists(1), "consts": consts_c if r == 0 else (lambda: None)}
+        lists(0)
+        for step in PLAN:
+            calls[step[0]](*step[1:])
+        if r == 0:
+            consts_b()
+
+        ts(A("SW", 0, 128, 16), K("LB"), K("I128", 0, 1), Op.add)
+        prev = K("L0")
+        for k in range(1, L):
+            o = 128 * (k % 2)
+            vgather(A("CM", o, o + 128), A("NXW"), prev, K("MK"), Op.mult)
+            scan(A("CS", o, o + 128), K("RS"), A("CM", o, o + 128), Op.mult, Op.add)
+            prev = A("LC", 8 * k, 8 * k + 8)
+            if k < L - 1:
+                cp(prev, A("CS", o + 15, o + 128, 16))
+            act(A("SW", k, 128, 16), A("CS", o + 15, o + 128, 16))
+        cp(A("LF"), A("SW"))
+        sgather(A("Xst"), A(X, 0, W), A("LF"))
+
+        tt(A("dif", 0, 127), A("SW", 1, 128), A("SW", 0, 127), Op.subtract)
+        ts(A("dif2", 0, 127), A("dif", 0, 127), W - 1, Op.bitwise_and)
+        ts(A("J", 0, 127), A("dif2", 0, 127), 1, Op.not_equal)
+        ms(A("J", 15, 128, 16), 0.0)
+        scan(A("INC"), K("ONF"), A("J"), Op.mult, Op.add)
+        mm(ps(6, 0, 1), K("LST1"), A("INC", 127, 128), True, True)
+        ts(A("ING"), A("INC"), ps(6, 0, 1), Op.add, 200.0, Op.min)
+        mm(ps(7, 0, 128), K("DSH"), A("ING"), True, True)
+        ts(A("GO"), K("NARR"), ps(6, 0, 1), Op.is_gt)
+        cp(A("DEL"), ps(7, 0, 128))
+        mm(ps(0, 0, 512), A("DEL"), A("GO", 0, 512), True, True)
+        mm(ps(1, 0, 128), A("DEL"), A("GO", 512, 640), True, True)
+        tt(A("CC", 0, 512), ps(0, 0, 512), K("NP1", 0, 512), Op.is_lt)
+        tt(A("CC", 512, 640), ps(1, 0, 128), K("NP1", 512, 640), Op.is_lt)
+        for d in range(ND):
+            mm(ps(2, 2 * d, 2 * d + 2), A("GO", 128 * d, 128 * d + 128), K("GW", 0, 2), True, False)
+            mm(ps(2, 2 * d, 2 * d + 2), A("CC", 128 * d, 128 * d + 128), K("CW", 0, 2), False, True)
+        ts(A("AL", 0, ND), ps(2, 0, 2 * ND, 2), -1.0, Op.add, float(W - 1), Op.min)
+        ak, qn = "ASK%d" % r, "QIN%d" % r
+        vgather(A(ak), A("Xst"), A("AL", 0, ND))
+        qs = [(Q * d, Q * d + Q) for d in range(ND)]
+        landed["q%d" % r] = send([A(ak, *x) for x in qs], [A(qn, *x) for x in qs], [cores[(rank + 1 + d) % N] for d in range(ND)], "q%d" % r)
+        ts(A("plc", 0, ND), ps(2, 1, 2 * ND, 2), -128.0, Op.add)
+        ts(A("live", 0, ND), A("plc", 0, ND), float(W), Op.is_lt)
+        ts(A("pl8", 0, ND), A("plc", 0, ND), 8193.0, Op.add)
+        mm(ps(6, 0, 128), K("ID16"), K("JJ"), True, False)
+        mm(ps(6, 0, 128), K("IDN"), K("ICOL"), False, False)
+
+        note([], [A(qn)], "q%d" % r, landed["q%d" % r])
+        mm(ps(3, 0, 80), A("WBLK"), A(qn), True, True)
+        act(A("QREP", 0, 80), A(qn))
+        act(A("QREP", 80, 160), A(qn))
+        act(A("QREP", 160, 320), A("QREP", 0, 160))
+        act(A("QREP", 320, 640), A("QREP", 0, 320))
+        act(A("QREP", 640, 960), A("QREP", 0, 320))
+        tt(A("VM"), ps(3, 0, 80), K("MK", 0, 80), Op.mult)
+        scan(A("VS"), K("RS", 0, 80), A("VM"), Op.mult, Op.add)
+        q = lambda n: A("q_" + n, 0, ND)
+        cp(q("vi"), A("VS", 15, 80, 16))
+        ts(q("va"), q("vi"), W - 1, Op.bitwise_and)
+        ts(q("vs"), q("vi"), W - 1, Op.bitwise_and, 5, Op.arith_shift_right)
+        ts(q("v2"), q("va"), 2, Op.mult)
+        tt(q("vb"), q("va"), q("vs"), Op.mult)
+        tt(q("c0"), q("vb"), q("va"), Op.add)
+        for d in range(ND):
+            ts(A("qraw", d, P * ND, ND), K("MC"), A("q_v2", d, d + 1), Op.mult, A("q_c0", d, d + 1), Op.add)
+        ts(A("qmsk"), A("qraw"), W - 1, Op.bitwise_and)
+        cp(A("qlst"), A("qmsk"))
+        parts = [(0, 60), (60, 120), (120, 160)]
+        gs[0] ^= 1
+        og = H * gs[0]
+        sgather(A("G", og, og + 640), A(X, 0, W), A("qlst", 120, 160))
+        for c in range(2):
+            mm(ps(1 - c, 0, 320), K("IDN"), A("G", og + 320 * c, og + 320 * c + 320), True, False)
+            mm(ps(1 - c, 0, 320), K("NEGI"), A("QREP", 0, 320), False, True)
+        for t in (0, 2, 1):
+            l0, l1 = parts[t]
+            n = 16 * (l1 - l0)
+            d, a, o = slot()
+            if t < 2:
+                vgather(A("D", o, o + n), A(X, 0, W), A("qlst", l0, l1), A("QREP", 0, n), Op.subtract)
+                act(A("AB", o, o + n), A("D", o, o + n), Fn.Abs)
+            else:
+                for c in range(2):
+                    act(A("AB", o + 320 * c, o + 320 * c + 320), ps(1 - c, 0, 320), Fn.Abs)
+            mm(ps(4, l0, l1), K("IDN"), K("MROW", l0, l1), True, False)
+            for i in range(16):
+                mm(ps(4, l0, l1), A("EI", 128 * i, 128 * i + 128), A("AB", o + i, o + n, 16), False, i == 15)
+        for d in range(ND):
+            a, b = A("q_KM", d, d + 1), ps(4, d, P * ND, ND)
+            do("V", lambda: g.vector.tensor_reduce(ap(a), ap(b), AxisListType.X, Op.min), [b], [a])
+        ts(q("ki"), q("KM"), float(P), Op.mult)
+        fl = "FIL%d" % r
+        ts(q("km"), q("ki"), P - 1, Op.bitwise_and)
+        tt(q("kt"), q("km"), q("v2"), Op.mult)
+        tt(q("kc"), q("kt"), q("c0"), Op.add)
+        ts(q("kd"), q("kc"), W - 1, Op.bitwise_and)
+        for f in range(F):
+            ts(A("FL", f, F * ND, F), q("kd"), f + 1, Op.add)
+        ts(A(fl, Q * F, ND * SLOT, SLOT), q("KM"), K("T", 1, 2), Op.is_lt)
+        for d in (0, 3, 1, 4, 2):
+            (sgather if d > 2 else vgather)(A(fl, SLOT * d, SLOT * d + Q * F), A(X, 0, W + 8), A("FL", F * d, F * d + F))
+        z = "ZIN%d" % r
+        zs = [(SLOT * d, SLOT * d + SLOT) for d in range(ND)]
+        landed["z%d" % r] = send([A(fl, *x) for x in zs], [A(z, *x) for x in zs], [cores[(rank - 1 - d) % N] for d in range(ND)], "z%d" % r)
+        for i in range(16):
+            act(A("Xnat", 128 * i, 128 * i + 128), A("Xst", i, W, 16))
+
+        note([], [A(z)], "z%d" % r, landed["z%d" % r])
+        tt(A("an", 0, ND), A(z, Q * F, ND * SLOT, SLOT), A("live", 0, ND), Op.mult)
+        mm(ps(5, 0, ND), K("LST6"), A("an", 0, ND), True, False)
+        for k in range(1, ND):
+            mm(ps(5, k, ND), K("BLK6"), A("an", 0, ND - k), False, False)
+        mm(ps(5, 0, ND), K("N8I"), A("an", 0, ND), False, True)
+        tt(A("a8", 0, ND), ps(5, 0, ND), A("pl8", 0, ND), Op.add)
+        ts(A("ahl", 0, ND), A("a8", 0, ND), 4, Op.arith_shift_right)
+        ts(A("ahl", 8, 8 + ND), A("a8", 0, ND), 15, Op.bitwise_and)
+        cp(A("ahf", 0, ND), A("ahl", 0, ND))
+        cp(A("ahf", 8, 8 + ND), A("ahl", 8, 8 + ND))
+        for d in range(ND):
+            o = 128 * d
+            hi, lo = A("ahf", d, d + 1), A("ahf", 8 + d, 9 + d)
+            ts(A("LT", o, o + 128), K("JJ"), hi, Op.is_gt)
+            ts(A("EQ", o, o + 128), K("JJ"), hi, Op.is_equal)
+            ts(A("LO", o, o + 128), K("IARR"), lo, Op.is_gt, -6.0, Op.mult)
+            mm(ps(6, 0, 128), K("NB6"), A("LT", o, o + 128), False, False)
+            mm(ps(6, 0, 128), A("LO", o, o + 128), A("EQ", o, o + 128), False, d == ND - 1)
+        for f in range(F):
+            ts(A("SL", f, F * ND, F), A("a8", 0, ND), f, Op.add)
+        tt(A("SL2", 0, 30), A("SL", 0, 30), K("JK", 0, 30), Op.min)
+        cp(A("SLu", 0, 30), A("SL2", 0, 30))
+        ts(A("PL", HJ, 2 * HJ), ps(6, HJ, 2 * HJ), 0.0, Op.max)
+        ts(A("PL", 0, HJ), ps(6, 0, HJ), 0.0, Op.max)
+        sgather(A(XN, H, W), A("Xnat"), A("PL", HJ, 2 * HJ))
+        vgather(A(XN, 0, H), A("Xnat"), A("PL", 0, HJ))
+        for d in range(ND):
+            scatter(A(XN), A("SLu", F * d, F * d + F), A(z, SLOT * d, SLOT * d + Q * F))
+        if r + 1 < RO:
+            act(A(XN, W, W + 8), A(XN, 0, 8))
+
+    dma("Y", T.y[:, 0:H], T.XC[:, 0:H], "dy0", [A("XC", 0, H)], [])
+    dma("S", T.y[:, H:W], T.XC[:, H:W], "dy1", [A("XC", H, W)], [])
+    for e in ("V", "S", "T", "G"):
+        wait("G", semof[e], cnt[e])
+    g.wait_ge(T.sem.lsem, tot[0])
+    for s in ("dwt", "dx0", "dx1", "dth", "dy0", "dy1"):
+        g.wait_ge(T.sem[s], 16)
+    for s in ("q0", "q1", "z0", "z1"):
+        g.wait_ge(T.sem[s], landed[s])

@@ -8,6 +8,7 @@ HJ = H // 16
 ND = N - 1
 SLOT = Q * F + 8
 RING = 6
+NG = 4
 XW = 3072
 
 SB = {}
@@ -31,10 +32,10 @@ def many(names, cols, dtype):
 
 
 many("XA XB XC", XW, "bfloat16")
-many("XP Xst Xnat WEI EI", W, "bfloat16")
+many("XP Xk Xst Xnat WEI EI", W, "bfloat16")
 sb("BIh", W, "float16")
 many("D AB", RING * H, "bfloat16")
-sb("G", 2 * H, "bfloat16")
+sb("G", NG * H, "bfloat16")
 many("i_ui i_ua i_us i_u2 i_r1 i_r2 i_nxw", 2 * HJ, "int32")
 many("raw msk", 2 * M * HJ, "int32")
 sb("lst", 2 * M * HJ, "uint16")
@@ -43,10 +44,11 @@ sb("RG", 2 * M * HJ, "bfloat16")
 many("f_r f_d f_e", 2 * HJ, "float32")
 sb("NXH", 2 * HJ, "float16")
 sb("NXW", W, "float32")
-many("CM CS", 256, "float32")
+many("CM CS", 256, "float16")
+many("k_RSh k_IDh k_NIh", 128, "float16")
+many("k_L0h k_ONh", 8, "float16")
 many("LC LF PL", 128, "uint16")
 many("SW J", 128, "float32")
-many("dif dif2", 128, "int32")
 many("INC ING DEL", 128, "bfloat16")
 many("GO CC EQ LT LO", 640, "bfloat16")
 sb("AL", 8, "uint16")
@@ -71,6 +73,7 @@ many("k_TMP k_BLK k_IDN k_LST1 k_LST6 k_BLK6 k_NB6 k_SHF k_DSH k_ID16 k_NEGI k_N
 many("k_NP1 k_NARRt k_NARR", 640, "bfloat16")
 sb("k_MROWf", P * ND, "float32")
 sb("k_MROW", P * ND, "bfloat16")
+sb("k_ZR", 16, "bfloat16")
 sb("k_MC", P, "float32")
 many("k_MKi k_MKa", 128, "int32")
 many("k_MK k_RS k_ONF k_PWb k_PW1", 128, "float32")
@@ -85,12 +88,12 @@ for _k in range(8):
 for _d in ARENA:
     SB[ARENA[_d][0]] = ("sbuf", [128, ARENA[_d][1]], _d)
 SCRATCH = SB
-SEMAPHORES = ["sV", "sS", "sT", "sG", "lsem", "dx0", "dx1", "dwt", "dth", "dy0", "dy1", "q0", "q1", "z0", "z1"]
+SEMAPHORES = ["sV", "sS", "sT", "sG", "lsem", "dx0", "dx1", "dwt", "dth", "dy0", "dy1", "q0", "q1", "z0", "z1"] + ["ga%d" % _k for _k in range(4 * RO)]
 
-WB = ((2, 7), (4, 5))
+WB = ((4, 5), (2, 3))
 PLAN = [tuple(int(c) if c.isdigit() else c for c in x.split(".")) for x in (
-    "v.0.0 v.0.2 lists v.0.3 sg.0.4 sub.0.4 v.1.2 v.1.1 a.0.0 a.0.2 sl.0.4 v.0.1 sg.1.4 sub.1.4 a.1.2 a.1.1 a.0.3 v.1.0 v.1.3 consts "
-    "a.0.1 sl.1.4 a.1.0 a.1.3 v.0.5 first.0 v.1.5 a.0.5 first.1 bl.0 a.1.5 succ.0 bl.1 succ.1 win.0 win.1").split()]
+    "sg.0.4 v.0.1 sg.0.3 lists v.0.0 a.0.1 sg.1.4 v.0.2 a.0.0 sl.0.4 v.1.0 a.0.2 sl.0.3 v.1.1 a.1.0 v.1.2 a.1.1 consts sl.1.4 v.1.3 "
+    "a.1.2 v.0.5 a.1.3 v.1.5 a.0.5 first.0 first.1 a.1.5 bl.0 succ.0 bl.1 succ.1 win.0 win.1").split()]
 
 
 def rank_program(g, core, T, topo):
@@ -176,9 +179,9 @@ def rank_program(g, core, T, topo):
         snap[(semof[e], cnt[e])] = dict(known[e])
         note(reads, writes, semof[e], cnt[e])
 
-    def dma(e, out, in_, sem, reads, writes):
+    def dma(e, out, in_, sem, reads, writes, **kw):
         need(e, reads, writes)
-        queue[e].dma_start(out=out, in_=in_).then_inc(T.sem[sem], 16)
+        queue[e].dma_start(out=out, in_=in_, **kw).then_inc(T.sem[sem], 16)
         snap[(sem, 16)] = dict(known[e])
         note(reads, writes, sem, 16)
 
@@ -207,8 +210,8 @@ def rank_program(g, core, T, topo):
     def scan(out, d0, d1, op0, op1):
         do("V", lambda: g.vector.tensor_tensor_scan(ap(out), ap(d0), ap(d1), 0.0, op0, op1), [d0, d1], [out])
 
-    def act(out, in_, func=Fn.Copy, scale=1.0):
-        do("S", lambda: g.scalar.activation(ap(out), ap(in_), func, scale=val(scale)), [in_] + ([scale] if is_ap(scale) else []), [out])
+    def act(out, in_, func=Fn.Copy, scale=1.0, bias=0.0):
+        do("S", lambda: g.scalar.activation(ap(out), ap(in_), func, bias=bias, scale=val(scale)), [in_] + ([scale] if is_ap(scale) else []), [out])
 
     def mm(out, l, r, start, stop):
         do("T", lambda: g.tensor.matmul(ap(out), ap(l), ap(r), start, stop), [l, r], [out])
@@ -219,8 +222,8 @@ def rank_program(g, core, T, topo):
         else:
             do("V", lambda: g.vector.tensor_tensor(ap(out), ap(win).indirect(ap(off)), ap(b), op), [win, off, b], [out])
 
-    def sgather(out, win, off):
-        do("S", lambda: g.scalar.activation(ap(out), ap(win).indirect(ap(off)), Fn.Copy), [win, off], [out])
+    def sgather(out, win, off, scale=1.0):
+        do("S", lambda: g.scalar.activation(ap(out), ap(win).indirect(ap(off)), Fn.Copy, scale=scale), [win, off], [out])
 
     def scatter(win, off, in_):
         do("V", lambda: g.vector.tensor_copy(ap(win).indirect(ap(off)), ap(in_)), [off, in_], [win])
@@ -236,7 +239,7 @@ def rank_program(g, core, T, topo):
 
     dma("Y", T.WT[:, 0:1], T.wt[:, :], "dwt", [], [A("WT", 0, 1)])
     dma("Y", T.XA[:, 0:H], T.x0[:, 0:H], "dx0", [], [A("XA", 0, H)])
-    dma("S", T.XA[:, H:W], T.x0[:, H:W], "dx1", [], [A("XA", H, W)])
+    dma("Y", T.XA[:, H:W], T.x0[:, H:W], "dx1", [], [A("XA", H, W)])
     dma("S", T.TH[:, 0:2], T.th[:, :], "dth", [], [A("TH", 0, 2)])
 
     K = lambda n, c0=0, c1=None, step=1: A("k_" + n, c0, c1, step)
@@ -248,9 +251,9 @@ def rank_program(g, core, T, topo):
     iota(K("PWb"), [[H, 2], [1, HJ]], 1, 0, True)
     iota(K("LB"), [[16, 8]], 0, 0, True)
     ms(A("WEI"), 0.0)
+    ms(A("EI"), 0.0)
     for i in range(16):
         ts(A("WEI", 128 * i + i, 128 * i + 128, 16), K("BLK", i, 128, 16), A("WT", 0, 1), Op.mult)
-    ms(A("EI"), 0.0)
     for i in range(16):
         act(A("EI", 128 * i + i, 128 * i + 128, 16), K("BLK", i, 128, 16))
     ts(K("p2", 0, 1), K("p", 0, 1), 15, Op.bitwise_and)
@@ -270,6 +273,12 @@ def rank_program(g, core, T, topo):
     cp(K("T", 0, 2), A("TH", 0, 2))
     ms(K("RS"), 1.0)
     ms(K("RS", 0, None, 16), 0.0)
+    cp(K("RSh"), K("RS"))
+    cp(K("IDh"), K("IDN"))
+    ts(K("NIh"), K("IDN"), -1.0, Op.mult)
+    ts(K("L0h"), K("LB"), K("I128", 0, 1), Op.add)
+    cp(K("ONh"), A("ONB", 0, 8))
+    ms(K("ZR"), 0.0)
     iota(K("NP1"), [[16, ND], [0, 8], [1, 16]], 1, 0, True)
     iota(K("JJ"), [[1, 128]], 0, 0, True)
     iota(K("IP1"), [[0, 8], [1, 16]], 1, 0, True)
@@ -297,32 +306,31 @@ def rank_program(g, core, T, topo):
     def consts_c():
         ms(K("ONF"), 1.0)
         tt(K("DSH"), K("IDN"), K("SHF"), Op.subtract)
-        ms(K("CW", 0, 1), 16.0)
+        ts(K("CW", 0, 1), K("MK", 15, 16), -2032.0, Op.mult, 128.0, Op.add)
         ms(K("CW", 1, 2), 1.0)
         ms(K("GW", 0, 1), 1.0)
         ms(K("GW", 1, 2), 128.0)
         ts(A("WBLK"), K("BLK"), A("WT", 0, 1), Op.mult)
         ts(K("JK", 0, 30), K("JKb", 0, 30), K("I16", 0, 1), Op.add)
 
-    def send(src, dst, dest, sem):
-        trs = []
-        for k in range(ND):
-            need("G", [src[k]], [])
-        for k in range(ND):
-            rid, pid = topo.addr(dest[k], core)
-            es = topo.engines(core, dest[k])
+    def send(src, dst, dest, sem, alone):
+        trs, order = [], [d for d in range(ND) if d != alone] + [alone]
+        for k, d in enumerate(order):
+            need("G", [src[d]], [])
+            rid, pid = topo.addr(dest[d], core)
+            es = topo.engines(core, dest[d])
             if k < 4:
                 n = len(es) // 4
                 mask = sum(1 << e for e in es[n * k:n * k + n])
                 trs.append(RemoteDMATransfer(dst_ids=[DstId(rid=rid, pnc=pid)], dma_engine_mask=mask, remote_sem=T.sem[sem],
-                                             src=ap(src[k]), dst=ap(dst[k])))
-                tot[0] += n
-        g.remote_dma_fused(trs, local_sem=T.sem.lsem)
-        g.remote_dma(ap(dst[4]), ap(src[4]), T.sem[sem], T.sem.lsem, pid, rid, topo.mask(core, dest[4]))
-        tot[0] += len(es)
+                                             src=ap(src[d]), dst=ap(dst[d])))
+                if k == 3:
+                    g.remote_dma_fused(trs, local_sem=T.sem.lsem)
+        g.remote_dma(ap(dst[alone]), ap(src[alone]), T.sem[sem], T.sem.lsem, pid, rid, topo.mask(core, dest[alone]))
+        tot[0] += 4 * n + len(es)
         return 4 * n + len(es)
 
-    tot, ring, gs, landed, place = [0], [0], [0], {}, {}
+    tot, ring, gs, landed, place, na = [0], [0], [0], {}, {}, [0]
     xs = ("XA", "XB", "XC")
     ps = lambda k, c0, c1, step=1: A("ps%d" % k, c0, c1, step)
     for r in range(RO):
@@ -339,14 +347,13 @@ def rank_program(g, core, T, topo):
         def lists(h):
             o, e = HJ * h, HJ * h + HJ
             ui, ua, us = [A("i_" + n, o, e) for n in ("ui", "ua", "us")]
-            u2, bb = ps(6, 128, 128 + HJ), ps(6, 256, 256 + HJ)
+            u2, bb = ps(6 + h, 128, 128 + HJ), ps(6 + h, 256, 256 + HJ)
             R = lambda m: A("raw", M * HJ * h + HJ * m, M * HJ * h + HJ * m + HJ)
             al = lambda n: A(n, M * HJ * h, M * HJ * h + M * HJ)
             cp(ui, ps(h, 0, HJ))
             ts(ua, ui, W - 1, Op.bitwise_and)
             ts(us, ui, W - 1, Op.bitwise_and, 5, Op.arith_shift_right)
             ts(u2, ua, 2, Op.mult)
-            ts(A("i_u2", o, e), ua, 2, Op.mult)
             tt(bb, ua, us, Op.mult)
             tt(R(0), bb, ua, Op.add)
             for m in range(1, M):
@@ -354,6 +361,7 @@ def rank_program(g, core, T, topo):
             ts(al("msk"), al("raw"), W - 1, Op.bitwise_and)
             cp(al("lst"), al("msk"))
             ts(A("i_r1", o, e), R(0), 1, Op.add)
+            ts(A("i_u2", o, e), ua, 2, Op.mult)
 
         def lk(h, m):
             return A("lst", M * HJ * h + HJ * m, M * HJ * h + HJ * m + HJ)
@@ -363,27 +371,26 @@ def rank_program(g, core, T, topo):
             o = H * (ring[0] % RING)
             return A("D", o, o + H), A("AB", o, o + H), o
 
+        def gslot(n):
+            gs[0] += 1
+            o = H * (gs[0] % NG)
+            return A("G", o, o + n)
+
         def dist(h, m, o):
             out = ps(2 + h, m, (M - 1) * HJ, M - 1) if m < M - 1 else ps(h, 0, HJ)
             for i in range(16):
                 mm(out, A("EI", 128 * i, 128 * i + 128), A("AB", o + i, o + H, 16), i == 0, i == 15)
 
         def sgath(h, m):
-            gs[0] ^= 1
-            o = H * gs[0]
-            sgather(A("G", o, o + H), A(X, 0, W), lk(h, m))
-            place["g", h, m] = o
-
-        def sub(h, m):
-            o = place["g", h, m]
-            for c in range(2):
-                mm(ps(4 + c, 0, 512), K("IDN"), A("G", o + 512 * c, o + 512 * c + 512), True, False)
-                mm(ps(4 + c, 0, 512), K("NEGI"), A("XP", H * h + 512 * c, H * h + 512 * c + 512), False, True)
+            a, b = gslot(H), A("XP", H * h, H * h + H)
+            place["g", h, m] = a
+            sgather(a, A(X, 0, W), lk(h, m), scale=-1.0)
+            dma("G", ap(a), ap(b), "ga%d" % na[0], [b], [a], accum_op=Op.add)
+            na[0] += 1
 
         def slook(h, m):
             d, a, o = slot()
-            for c in range(2):
-                act(A("AB", o + 512 * c, o + 512 * c + 512), ps(4 + c, 0, 512), Fn.Abs)
+            act(a, place["g", h, m], Fn.Abs)
             dist(h, m, o)
 
         def vlook(h, m):
@@ -397,23 +404,23 @@ def rank_program(g, core, T, topo):
             dist(h, m, o)
 
         def first(h):
-            o, n, s, e = M * HJ * h, (M - 1) * HJ, HJ * h, HJ * h + HJ
+            o, n = M * HJ * h, (M - 1) * HJ
             scan(A("RUN", o, o + n), K("RB5"), ps(2 + h, 0, n), Op.add, Op.min)
             ts(A("RG", o, o + n), A("RUN", o, o + n), K("T", 0, 1), Op.is_ge)
             for m in range(M - 1):
-                mm(ps(6, s, e), K("IDN"), A("RG", o + m, o + n, M - 1), m == 0, m == M - 2)
+                mm(ps(6 + h, 0, HJ), K("IDN"), A("RG", o + m, o + n, M - 1), m == 0, m == M - 2)
 
         def before_last(h):
             o, n, s, e = M * HJ * h, (M - 1) * HJ, HJ * h, HJ * h + HJ
-            ft, fd = ps(6, 128 + s, 128 + e), ps(6, 256 + s, 256 + e)
-            tt(ft, ps(6, s, e), A("i_u2", s, e), Op.mult)
+            ft, fd = ps(6 + h, 128, 128 + HJ), ps(6 + h, 256, 256 + HJ)
+            tt(ft, ps(6 + h, 0, HJ), A("i_u2", s, e), Op.mult)
             tt(A("f_r", s, e), ft, A("i_r1", s, e), Op.add)
             tt(fd, K("PW1", s, e), A("f_r", s, e), Op.subtract)
             tt(A("f_e", s, e), fd, A("RG", o + M - 2, o + n, M - 1), Op.mult)
 
         def succ(h):
             s, e = HJ * h, HJ * h + HJ
-            ft = ps(6, 128 + s, 128 + e)
+            ft = ps(6 + h, 128, 128 + HJ)
             ts(ft, ps(h, 0, HJ), K("T", 0, 1), Op.is_ge)
             tt(A("f_d", s, e), ft, A("f_e", s, e), Op.mult)
             tt(A("i_r2", s, e), A("f_r", s, e), A("f_d", s, e), Op.add)
@@ -426,7 +433,7 @@ def rank_program(g, core, T, topo):
             act(A("NXW", H * h, H * h + 512), ps(WB[h][0], 0, 512))
             cp(A("NXW", H * h + 512, H * h + H), ps(WB[h][1], 0, 512))
 
-        calls = {"sg": sgath, "sub": sub, "sl": slook, "v": vlook, "a": size, "first": first, "bl": before_last, "succ": succ,
+        calls = {"sg": sgath, "sl": slook, "v": vlook, "a": size, "first": first, "bl": before_last, "succ": succ,
                  "win": window, "lists": lambda: lists(1), "consts": consts_c if r == 0 else (lambda: None)}
         lists(0)
         for step in PLAN:
@@ -434,41 +441,47 @@ def rank_program(g, core, T, topo):
         if r == 0:
             consts_b()
 
-        ts(A("SW", 0, 128, 16), K("LB"), K("I128", 0, 1), Op.add)
-        prev = K("L0")
+        mm(ps(7, 15, 128, 16), K("IDh"), K("ONh"), True, True)
+        mm(ps(3, 0, 128, 16), K("IDh"), K("L0h"), True, True)
+        prev, last = K("L0"), K("L0h")
+        sgather(A("Xk", 0, 128), A(X, 0, W), prev)
         for k in range(1, L):
             o = 128 * (k % 2)
             vgather(A("CM", o, o + 128), A("NXW"), prev, K("MK"), Op.mult)
-            scan(A("CS", o, o + 128), K("RS"), A("CM", o, o + 128), Op.mult, Op.add)
+            scan(A("CS", o, o + 128), K("RSh"), A("CM", o, o + 128), Op.mult, Op.add)
             prev = A("LC", 8 * k, 8 * k + 8)
-            if k < L - 1:
-                cp(prev, A("CS", o + 15, o + 128, 16))
-            act(A("SW", k, 128, 16), A("CS", o + 15, o + 128, 16))
-        cp(A("LF"), A("SW"))
+            now = A("CS", o + 15, o + 128, 16)
+            cp(prev, now)
+            mm(ps(3, k, 128, 16), K("IDh"), now, True, True)
+            mm(ps(7, k - 1, 128, 16), K("NIh"), last, True, False)
+            mm(ps(7, k - 1, 128, 16), K("IDh"), now, False, True)
+            last = now
+            if k == L - 1:
+                cp(A("LF"), ps(3, 0, 128))
+                act(A("SW"), ps(7, 0, 128), Fn.Abs, bias=1023.0)
+            sgather(A("Xk", 128 * k, 128 * k + 128), A(X, 0, W), prev)
         sgather(A("Xst"), A(X, 0, W), A("LF"))
 
-        tt(A("dif", 0, 127), A("SW", 1, 128), A("SW", 0, 127), Op.subtract)
-        ts(A("dif2", 0, 127), A("dif", 0, 127), W - 1, Op.bitwise_and)
-        ts(A("J", 0, 127), A("dif2", 0, 127), 1, Op.not_equal)
-        ms(A("J", 15, 128, 16), 0.0)
+        ts(A("J"), A("SW"), 1024.0, Op.not_equal)
+        mm(ps(2, 0, 2 * ND), K("IDN"), K("ZR", 0, 2 * ND), True, False)
         scan(A("INC"), K("ONF"), A("J"), Op.mult, Op.add)
         mm(ps(6, 0, 1), K("LST1"), A("INC", 127, 128), True, True)
         ts(A("ING"), A("INC"), ps(6, 0, 1), Op.add, 200.0, Op.min)
         mm(ps(7, 0, 128), K("DSH"), A("ING"), True, True)
         ts(A("GO"), K("NARR"), ps(6, 0, 1), Op.is_gt)
         cp(A("DEL"), ps(7, 0, 128))
-        mm(ps(0, 0, 512), A("DEL"), A("GO", 0, 512), True, True)
-        mm(ps(1, 0, 128), A("DEL"), A("GO", 512, 640), True, True)
-        tt(A("CC", 0, 512), ps(0, 0, 512), K("NP1", 0, 512), Op.is_lt)
-        tt(A("CC", 512, 640), ps(1, 0, 128), K("NP1", 512, 640), Op.is_lt)
-        for d in range(ND):
-            mm(ps(2, 2 * d, 2 * d + 2), A("GO", 128 * d, 128 * d + 128), K("GW", 0, 2), True, False)
-            mm(ps(2, 2 * d, 2 * d + 2), A("CC", 128 * d, 128 * d + 128), K("CW", 0, 2), False, True)
-        ts(A("AL", 0, ND), ps(2, 0, 2 * ND, 2), -1.0, Op.add, float(W - 1), Op.min)
+        for c in range(2):
+            mm(ps(c, 0, 320), A("DEL"), A("GO", 320 * c, 320 * c + 320), True, True)
+        for c in range(2):
+            tt(A("CC", 320 * c, 320 * c + 320), ps(c, 0, 320), K("NP1", 320 * c, 320 * c + 320), Op.is_lt)
+        for s, w in (("GO", "GW"), ("CC", "CW")):
+            for d in range(ND):
+                mm(ps(2, 2 * d, 2 * d + 2), A(s, 128 * d, 128 * d + 128), K(w, 0, 2), False, s == "CC" and d == ND - 1)
+        ts(A("AL", 0, ND), ps(2, 0, 2 * ND, 2), -1.0, Op.add)
         ak, qn = "ASK%d" % r, "QIN%d" % r
-        vgather(A(ak), A("Xst"), A("AL", 0, ND))
+        vgather(A(ak), A("Xk"), A("AL", 0, ND))
         qs = [(Q * d, Q * d + Q) for d in range(ND)]
-        landed["q%d" % r] = send([A(ak, *x) for x in qs], [A(qn, *x) for x in qs], [cores[(rank + 1 + d) % N] for d in range(ND)], "q%d" % r)
+        landed["q%d" % r] = send([A(ak, *x) for x in qs], [A(qn, *x) for x in qs], [cores[(rank + 1 + d) % N] for d in range(ND)], "q%d" % r, ND - 1)
         ts(A("plc", 0, ND), ps(2, 1, 2 * ND, 2), -128.0, Op.add)
         ts(A("live", 0, ND), A("plc", 0, ND), float(W), Op.is_lt)
         ts(A("pl8", 0, ND), A("plc", 0, ND), 8193.0, Op.add)
@@ -496,11 +509,10 @@ def rank_program(g, core, T, topo):
         ts(A("qmsk"), A("qraw"), W - 1, Op.bitwise_and)
         cp(A("qlst"), A("qmsk"))
         parts = [(0, 60), (60, 120), (120, 160)]
-        gs[0] ^= 1
-        og = H * gs[0]
-        sgather(A("G", og, og + 640), A(X, 0, W), A("qlst", 120, 160))
+        gb = gslot(640)
+        sgather(gb, A(X, 0, W), A("qlst", 120, 160))
         for c in range(2):
-            mm(ps(1 - c, 0, 320), K("IDN"), A("G", og + 320 * c, og + 320 * c + 320), True, False)
+            mm(ps(1 - c, 0, 320), K("IDN"), A("G", gb[1] + 320 * c, gb[1] + 320 * c + 320), True, False)
             mm(ps(1 - c, 0, 320), K("NEGI"), A("QREP", 0, 320), False, True)
         for t in (0, 2, 1):
             l0, l1 = parts[t]
@@ -531,7 +543,7 @@ def rank_program(g, core, T, topo):
             (sgather if d > 2 else vgather)(A(fl, SLOT * d, SLOT * d + Q * F), A(X, 0, W + 8), A("FL", F * d, F * d + F))
         z = "ZIN%d" % r
         zs = [(SLOT * d, SLOT * d + SLOT) for d in range(ND)]
-        landed["z%d" % r] = send([A(fl, *x) for x in zs], [A(z, *x) for x in zs], [cores[(rank - 1 - d) % N] for d in range(ND)], "z%d" % r)
+        landed["z%d" % r] = send([A(fl, *x) for x in zs], [A(z, *x) for x in zs], [cores[(rank - 1 - d) % N] for d in range(ND)], "z%d" % r, 2)
         for i in range(16):
             act(A("Xnat", 128 * i, 128 * i + 128), A("Xst", i, W, 16))
 
@@ -543,12 +555,11 @@ def rank_program(g, core, T, topo):
         mm(ps(5, 0, ND), K("N8I"), A("an", 0, ND), False, True)
         tt(A("a8", 0, ND), ps(5, 0, ND), A("pl8", 0, ND), Op.add)
         ts(A("ahl", 0, ND), A("a8", 0, ND), 4, Op.arith_shift_right)
-        ts(A("ahl", 8, 8 + ND), A("a8", 0, ND), 15, Op.bitwise_and)
-        cp(A("ahf", 0, ND), A("ahl", 0, ND))
-        cp(A("ahf", 8, 8 + ND), A("ahl", 8, 8 + ND))
+        ts(A("ahl", ND, 2 * ND), A("a8", 0, ND), 15, Op.bitwise_and)
+        cp(A("ahf", 0, 2 * ND), A("ahl", 0, 2 * ND))
         for d in range(ND):
             o = 128 * d
-            hi, lo = A("ahf", d, d + 1), A("ahf", 8 + d, 9 + d)
+            hi, lo = A("ahf", d, d + 1), A("ahf", ND + d, ND + d + 1)
             ts(A("LT", o, o + 128), K("JJ"), hi, Op.is_gt)
             ts(A("EQ", o, o + 128), K("JJ"), hi, Op.is_equal)
             ts(A("LO", o, o + 128), K("IARR"), lo, Op.is_gt, -6.0, Op.mult)

import numpy as np
from concourse.bass import DstId, RemoteDMATransfer
from concourse.mybir import dt, AluOpType as Op, AxisListType, ActivationFunctionType as Fn

N, W, L, M, P, Q, F, RO = 6, 2048, 16, 6, 32, 16, 6, 2
H = W // 2
HJ = H // 16
ND = N - 1
SLOT = Q * F + 8
RING = 6
NG = 4
XW = 3072

SB = {}
PART = {}
ARENA = {"int32": ["ar_i", 0], "float32": ["ar_f", 0], "bfloat16": ["ar_b", 0], "uint16": ["ar_u", 0]}
OWN = ("WT", "TH")


def sb(name, cols, dtype):
    if cols <= 160 and dtype in ARENA and name not in OWN and not name.startswith(("QIN", "ASK")):
        a = ARENA[dtype]
        PART[name] = (a[0], a[1], cols)
        a[1] += -(-cols // 16) * 16
    else:
        SB[name] = ("sbuf", [128, cols], dtype)


def many(names, cols, dtype):
    for n in names.split():
        sb(n, cols, dtype)


many("XA XB XC", XW, "bfloat16")
many("XP Xk Xst Xnat WEI EI", W, "bfloat16")
sb("BIh", W, "float16")
many("D AB", RING * H, "bfloat16")
sb("G", NG * H, "bfloat16")
many("i_ui i_ua i_us i_u2 i_r1 i_r2 i_nxw", 2 * HJ, "int32")
many("raw msk", 2 * M * HJ, "int32")
sb("lst", 2 * M * HJ, "uint16")
sb("RUN", 2 * M * HJ, "float32")
sb("RG", 2 * M * HJ, "bfloat16")
many("f_r f_d f_e", 2 * HJ, "float32")
sb("NXH", 2 * HJ, "float16")
sb("NXW", W, "float32")
many("CM CS", 256, "float16")
many("k_RSh k_IDh k_NIh", 128, "float16")
many("k_L0h k_ONh", 8, "float16")
many("LC LF PL", 128, "uint16")
many("SW J", 128, "float32")
many("INC ING DEL", 128, "bfloat16")
many("GO CC EQ LT LO", 640, "bfloat16")
sb("AL", 8, "uint16")
many("plc live pl8", 8, "float32")
for _r in range(RO):
    many("ASK%d QIN%d" % (_r, _r), ND * Q, "bfloat16")
    many("FIL%d ZIN%d" % (_r, _r), ND * SLOT, "bfloat16")
sb("QREP", 12 * ND * Q, "bfloat16")
many("VM VS", 80, "float32")
many("q_vi q_va q_vs q_vb q_ki q_km q_kc q_kd", 8, "int32")
many("q_c0 q_v2 q_KM q_kt", 8, "float32")
many("qraw qmsk", P * ND, "int32")
sb("qlst", P * ND, "uint16")
many("FL SLu", 32, "uint16")
sb("an", 8, "bfloat16")
sb("a8", 8, "int32")
sb("ahl", 16, "int32")
sb("ahf", 16, "float32")
many("SL SL2", 32, "float32")
many("ONB WBLK", 128, "bfloat16")
many("k_TMP k_BLK k_IDN k_LST1 k_LST6 k_BLK6 k_NB6 k_SHF k_DSH k_ID16 k_NEGI k_N8I k_JJ k_IP1 k_IARRt k_IARR k_ICOL", 128, "bfloat16")
many("k_NP1 k_NARRt k_NARR", 640, "bfloat16")
sb("k_MROWf", P * ND, "float32")
sb("k_MROW", P * ND, "bfloat16")
sb("k_ZR", 16, "bfloat16")
sb("k_MC", P, "float32")
many("k_MKi k_MKa", 128, "int32")
many("k_MK k_RS k_ONF k_PWb k_PW1", 128, "float32")
sb("k_RB5", (M - 1) * HJ, "float32")
many("k_p k_p2 TH", 8, "int32")
many("k_I16 k_I64 k_I128 k_LB k_T", 8, "float32")
sb("k_L0", 8, "uint16")
many("k_CW k_GW WT", 8, "bfloat16")
many("k_JKb k_JK", 32, "float32")
for _k in range(8):
    SB["ps%d" % _k] = ("psum", [128, 512], "float32")
for _d in ARENA:
    SB[ARENA[_d][0]] = ("sbuf", [128, ARENA[_d][1]], _d)
SCRATCH = SB
SEMAPHORES = ["sV", "sS", "sT", "sG", "lsem", "dx0", "dx1", "dwt", "dth", "dy0", "dy1", "q0", "q1", "z0", "z1"] + ["ga%d" % _k for _k in range(4 * RO)]

WB = ((4, 5), (2, 3))
PLAN = [tuple(int(c) if c.isdigit() else c for c in x.split(".")) for x in (
    "sg.0.4 v.0.1 sg.0.3 lists v.0.0 a.0.1 sg.1.4 v.0.2 a.0.0 sl.0.4 v.1.0 a.0.2 sl.0.3 v.1.1 a.1.0 v.1.2 a.1.1 consts sl.1.4 v.1.3 "
    "a.1.2 v.0.5 a.1.3 v.1.5 a.0.5 first.0 first.1 a.1.5 bl.0 succ.0 bl.1 succ.1 win.0 win.1").split()]


def rank_program(g, core, T, topo):
    rank = T.rank_of(core)
    if rank is None:
        return
    cores = T.cores
    queue = {"V": g.vector, "S": g.scalar, "T": g.tensor, "G": g, "Y": g.sync}
    semof = {"V": "sV", "S": "sS", "T": "sT", "G": "sG"}
    cnt = {"V": 0, "S": 0, "T": 0, "G": 0}
    known = {"V": {}, "S": {}, "T": {}, "G": {}, "Y": {}}
    snap = {}
    log = {}

    def A(name, c0=0, c1=None, step=1):
        if name in PART:
            a, o, n = PART[name]
            return (a, o + c0, o + (n if c1 is None else c1), step)
        n = SB[name][1][1]
        return (name, c0, n if c1 is None else c1, step)

    def ap(a):
        return T[a[0]][:, a[1]:a[2]:a[3]] if a[3] != 1 else T[a[0]][:, a[1]:a[2]]

    def overlap(a, b):
        if a[1] >= b[2] or b[1] >= a[2]:
            return False
        if a[3] == b[3] and a[3] > 1 and (a[1] - b[1]) % a[3]:
            return False
        return True

    def wait(e, sem, val):
        k = known[e]
        if k.get(sem, 0) >= val:
            return
        queue[e].wait_ge(T.sem[sem], val)
        s = snap.get((sem, val))
        if s:
            for q in s:
                if s[q] > k.get(q, 0):
                    k[q] = s[q]
        k[sem] = val

    def need(e, reads, writes):
        own = semof.get(e)
        req = {}
        for lst, isw in ((reads, False), (writes, True)):
            for a in lst:
                ps = SB[a[0]][0] == "psum"
                for (w, b, sem, val) in log.get(a[0], ()):
                    if sem == own:
                        if not w or (ps and e == "T" and isw) or not overlap(a, b):
                            continue
                    elif not ps:
                        if not (w or isw) or not overlap(a, b):
                            continue
                    if val > req.get(sem, 0):
                        req[sem] = val
        for s in sorted(req, key=lambda s: -req[s]):
            wait(e, s, req[s])

    def covers(a, b):
        return a[1] <= b[1] and a[2] >= b[2] and (a[3] == 1 or (a[3] == b[3] and (a[1] - b[1]) % a[3] == 0))

    def note(reads, writes, sem, val):
        for a in writes:
            l = log.get(a[0], [])
            if SB[a[0]][0] != "psum":
                l = [x for x in l if not covers(a, x[1])]
            else:
                l = [x for x in l if not (x[0] and x[2] == sem and covers(a, x[1]))]
            l.append((True, a, sem, val))
            log[a[0]] = l
        for a in reads:
            l = log.setdefault(a[0], [])
            l[:] = [x for x in l if x[0] or x[2] != sem or not covers(a, x[1])]
            l.append((False, a, sem, val))

    def do(e, fn, reads, writes):
        need(e, reads, writes)
        cnt[e] += 1
        fn().then_inc(T.sem[semof[e]], 1)
        snap[(semof[e], cnt[e])] = dict(known[e])
        note(reads, writes, semof[e], cnt[e])

    def dma(e, out, in_, sem, reads, writes, **kw):
        need(e, reads, writes)
        queue[e].dma_start(out=out, in_=in_, **kw).then_inc(T.sem[sem], 16)
        snap[(sem, 16)] = dict(known[e])
        note(reads, writes, sem, 16)

    def is_ap(x):
        return isinstance(x, tuple)

    def val(x):
        return ap(x) if is_ap(x) else x

    def cp(out, in_):
        do("V", lambda: g.vector.tensor_copy(ap(out), ap(in_)), [in_], [out])

    def tt(out, a, b, op):
        do("V", lambda: g.vector.tensor_tensor(ap(out), ap(a), ap(b), op), [a, b], [out])

    def ts(out, a, s1, op0, s2=None, op1=None):
        rd = [a] + [s for s in (s1, s2) if is_ap(s)]
        if op1 is None:
            do("V", lambda: g.vector.tensor_scalar(ap(out), ap(a), val(s1), None, op0), rd, [out])
        else:
            do("V", lambda: g.vector.tensor_scalar(ap(out), ap(a), val(s1), val(s2), op0, op1), rd, [out])

    def ms(out, c):
        do("V", lambda: g.vector.memset(ap(out), c), [], [out])

    def scan(out, d0, d1, op0, op1):
        do("V", lambda: g.vector.tensor_tensor_scan(ap(out), ap(d0), ap(d1), 0.0, op0, op1), [d0, d1], [out])

    def act(out, in_, func=Fn.Copy, scale=1.0, bias=0.0):
        do("S", lambda: g.scalar.activation(ap(out), ap(in_), func, bias=bias, scale=val(scale)), [in_] + ([scale] if is_ap(scale) else []), [out])

    def mm(out, l, r, start, stop):
        do("T", lambda: g.tensor.matmul(ap(out), ap(l), ap(r), start, stop), [l, r], [out])

    def vgather(out, win, off, b=None, op=None):
        if b is None:
            do("V", lambda: g.vector.tensor_copy(ap(out), ap(win).indirect(ap(off))), [win, off], [out])
        else:
            do("V", lambda: g.vector.tensor_tensor(ap(out), ap(win).indirect(ap(off)), ap(b), op), [win, off, b], [out])

    def sgather(out, win, off, scale=1.0):
        do("S", lambda: g.scalar.activation(ap(out), ap(win).indirect(ap(off)), Fn.Copy, scale=scale), [win, off], [out])

    def scatter(win, off, in_):
        do("V", lambda: g.vector.tensor_copy(ap(win).indirect(ap(off)), ap(in_)), [off, in_], [win])

    def iota(out, pattern, base, chan, flag=False):
        if flag:
            do("G", lambda: g.iota(ap(out), pattern, base, chan, allow_small_or_imprecise_dtypes=True), [], [out])
        else:
            do("G", lambda: g.iota(ap(out), pattern, base, chan), [], [out])

    def asel(out, in_, pattern, op, base, chan):
        do("G", lambda: g.affine_select(ap(out), ap(in_), pattern, op, 0.0, base, chan), [in_], [out])

    dma("Y", T.WT[:, 0:1], T.wt[:, :], "dwt", [], [A("WT", 0, 1)])
    dma("Y", T.XA[:, 0:H], T.x0[:, 0:H], "dx0", [], [A("XA", 0, H)])
    dma("Y", T.XA[:, H:W], T.x0[:, H:W], "dx1", [], [A("XA", H, W)])
    dma("S", T.TH[:, 0:2], T.th[:, :], "dth", [], [A("TH", 0, 2)])

    K = lambda n, c0=0, c1=None, step=1: A("k_" + n, c0, c1, step)
    ms(A("ONB"), 1.0)
    asel(K("TMP"), A("ONB"), [[-16, 8], [0, 16]], Op.is_ge, 0, 1)
    asel(K("BLK"), K("TMP"), [[16, 8], [0, 16]], Op.is_ge, 15, -1)
    iota(K("p", 0, 1), [[0, 1]], 0, 1)
    iota(K("MKi"), [[-1, 128]], 128, 1)
    iota(K("PWb"), [[H, 2], [1, HJ]], 1, 0, True)
    iota(K("LB"), [[16, 8]], 0, 0, True)
    ms(A("WEI"), 0.0)
    ms(A("EI"), 0.0)
    for i in range(16):
        ts(A("WEI", 128 * i + i, 128 * i + 128, 16), K("BLK", i, 128, 16), A("WT", 0, 1), Op.mult)
    for i in range(16):
        act(A("EI", 128 * i + i, 128 * i + 128, 16), K("BLK", i, 128, 16))
    ts(K("p2", 0, 1), K("p", 0, 1), 15, Op.bitwise_and)
    cp(K("I16", 0, 1), K("p2", 0, 1))
    ts(K("I64", 0, 1), K("I16", 0, 1), float(HJ), Op.mult)
    ts(K("I128", 0, 1), K("I16", 0, 1), 128.0, Op.mult)
    ts(K("PW1"), K("PWb"), K("I64", 0, 1), Op.add)
    ts(K("L0"), K("LB"), K("I128", 0, 1), Op.add)
    ts(K("MKa"), K("MKi"), 15, Op.bitwise_and)
    ts(K("MK"), K("MKa"), 0, Op.is_equal)
    asel(K("IDN"), A("ONB"), [[-1, 128]], Op.is_equal, 0, 1)
    ts(K("NEGI"), K("IDN"), -1.0, Op.mult)
    for i in range(16):
        ts(A("BIh", 128 * i, 128 * i + 128), K("BLK"), K("MK", i, i + 1), Op.mult)
    ms(K("RB5"), 0.0)
    ms(K("RB5", 0, None, M - 1), 100000.0)
    cp(K("T", 0, 2), A("TH", 0, 2))
    ms(K("RS"), 1.0)
    ms(K("RS", 0, None, 16), 0.0)
    cp(K("RSh"), K("RS"))
    cp(K("IDh"), K("IDN"))
    ts(K("NIh"), K("IDN"), -1.0, Op.mult)
    ts(K("L0h"), K("LB"), K("I128", 0, 1), Op.add)
    cp(K("ONh"), A("ONB", 0, 8))
    ms(K("ZR"), 0.0)
    iota(K("NP1"), [[16, ND], [0, 8], [1, 16]], 1, 0, True)
    iota(K("JJ"), [[1, 128]], 0, 0, True)
    iota(K("IP1"), [[0, 8], [1, 16]], 1, 0, True)
    iota(K("MC"), [[1, P]], 0, 0, True)
    iota(K("MROWf"), [[1, P], [0, ND]], 0, 0, True)
    iota(K("JKb", 0, 30), [[16, 30]], 2560, 0, True)
    asel(K("LST1"), K("BLK"), [[1, 128]], Op.is_ge, -1, -1)
    asel(K("SHF"), K("BLK"), [[1, 128]], Op.is_equal, -1, -1)
    asel(K("NARRt"), K("NP1"), [[0, ND], [-16, 8], [0, 16]], Op.is_ge, 0, 1)
    asel(K("NARR"), K("NARRt"), [[0, ND], [16, 8], [0, 16]], Op.is_ge, 15, -1)
    asel(K("IARRt"), K("IP1"), [[-16, 8], [0, 16]], Op.is_ge, 0, 1)
    asel(K("IARR"), K("IARRt"), [[16, 8], [0, 16]], Op.is_ge, 15, -1)

    def consts_b():
        act(K("MROW"), K("MROWf"), scale=1.0 / P)
        act(K("LST6"), K("LST1"), scale=6.0)
        act(K("BLK6"), K("BLK"), scale=6.0)
        act(K("NB6"), K("BLK"), scale=-6.0)
        act(K("ID16"), K("IDN"), scale=16.0)
        act(K("N8I"), K("IDN"), scale=-8192.0)
        act(K("ICOL"), A("ONB"), scale=K("I16", 0, 1))
        for r in range(RO):
            act(A("FIL%d" % r), K("NARR", 0, ND * SLOT), scale=0.0)

    def consts_c():
        ms(K("ONF"), 1.0)
        tt(K("DSH"), K("IDN"), K("SHF"), Op.subtract)
        ts(K("CW", 0, 1), K("MK", 15, 16), -2032.0, Op.mult, 128.0, Op.add)
        ms(K("CW", 1, 2), 1.0)
        ms(K("GW", 0, 1), 1.0)
        ms(K("GW", 1, 2), 128.0)
        ts(A("WBLK"), K("BLK"), A("WT", 0, 1), Op.mult)
        ts(K("JK", 0, 30), K("JKb", 0, 30), K("I16", 0, 1), Op.add)

    def send(src, dst, dest, sem, alone):
        trs, order = [], [d for d in range(ND) if d != alone] + [alone]
        for k, d in enumerate(order):
            need("G", [src[d]], [])
            rid, pid = topo.addr(dest[d], core)
            es = topo.engines(core, dest[d])
            if k < 4:
                n = len(es) // 4
                mask = sum(1 << e for e in es[n * k:n * k + n])
                trs.append(RemoteDMATransfer(dst_ids=[DstId(rid=rid, pnc=pid)], dma_engine_mask=mask, remote_sem=T.sem[sem],
                                             src=ap(src[d]), dst=ap(dst[d])))
                if k == 3:
                    g.remote_dma_fused(trs, local_sem=T.sem.lsem)
        g.remote_dma(ap(dst[alone]), ap(src[alone]), T.sem[sem], T.sem.lsem, pid, rid, topo.mask(core, dest[alone]))
        tot[0] += 4 * n + len(es)
        return 4 * n + len(es)

    tot, ring, gs, landed, place, na = [0], [0], [0], {}, {}, [0]
    xs = ("XA", "XB", "XC")
    ps = lambda k, c0, c1, step=1: A("ps%d" % k, c0, c1, step)
    for r in range(RO):
        X, XN = xs[r], xs[r + 1]

        for h in range(2):
            for i in range(16):
                mm(ps(h, 0, HJ), A("WEI", 128 * i, 128 * i + 128), A(X, H * h + HJ * i, H * h + HJ * i + HJ), i == 0, i == 15)
            for i in range(16):
                act(A("XP", H * h + i, H * h + H, 16), A(X, H * h + HJ * i, H * h + HJ * i + HJ))
        if r == 0:
            act(A(X, W, W + 8), A(X, 0, 8))

        def lists(h):
            o, e = HJ * h, HJ * h + HJ
            ui, ua, us = [A("i_" + n, o, e) for n in ("ui", "ua", "us")]
            u2, bb = ps(6 + h, 128, 128 + HJ), ps(6 + h, 256, 256 + HJ)
            R = lambda m: A("raw", M * HJ * h + HJ * m, M * HJ * h + HJ * m + HJ)
            al = lambda n: A(n, M * HJ * h, M * HJ * h + M * HJ)
            cp(ui, ps(h, 0, HJ))
            ts(ua, ui, W - 1, Op.bitwise_and)
            ts(us, ui, W - 1, Op.bitwise_and, 5, Op.arith_shift_right)
            ts(u2, ua, 2, Op.mult)
            tt(bb, ua, us, Op.mult)
            tt(R(0), bb, ua, Op.add)
            for m in range(1, M):
                tt(R(m), u2, R(m - 1), Op.add)
            ts(al("msk"), al("raw"), W - 1, Op.bitwise_and)
            cp(al("lst"), al("msk"))
            ts(A("i_r1", o, e), R(0), 1, Op.add)
            ts(A("i_u2", o, e), ua, 2, Op.mult)

        def lk(h, m):
            return A("lst", M * HJ * h + HJ * m, M * HJ * h + HJ * m + HJ)

        def slot():
            ring[0] += 1
            o = H * (ring[0] % RING)
            return A("D", o, o + H), A("AB", o, o + H), o

        def gslot(n):
            gs[0] += 1
            o = H * (gs[0] % NG)
            return A("G", o, o + n)

        def dist(h, m, o):
            out = ps(2 + h, m, (M - 1) * HJ, M - 1) if m < M - 1 else ps(h, 0, HJ)
            for i in range(16):
                mm(out, A("EI", 128 * i, 128 * i + 128), A("AB", o + i, o + H, 16), i == 0, i == 15)

        def sgath(h, m):
            a, b = gslot(H), A("XP", H * h, H * h + H)
            place["g", h, m] = a
            sgather(a, A(X, 0, W), lk(h, m), scale=-1.0)
            dma("G", ap(a), ap(b), "ga%d" % na[0], [b], [a], accum_op=Op.add)
            na[0] += 1

        def slook(h, m):
            d, a, o = slot()
            act(a, place["g", h, m], Fn.Abs)
            dist(h, m, o)

        def vlook(h, m):
            d, a, o = slot()
            place[h, m] = d, a, o
            vgather(d, A(X, 0, W), lk(h, m), A("XP", H * h, H * h + H), Op.subtract)

        def size(h, m):
            d, a, o = place[h, m]
            act(a, d, Fn.Abs)
            dist(h, m, o)

        def first(h):
            o, n = M * HJ * h, (M - 1) * HJ
            scan(A("RUN", o, o + n), K("RB5"), ps(2 + h, 0, n), Op.add, Op.min)
            ts(A("RG", o, o + n), A("RUN", o, o + n), K("T", 0, 1), Op.is_ge)
            for m in range(M - 1):
                mm(ps(6 + h, 0, HJ), K("IDN"), A("RG", o + m, o + n, M - 1), m == 0, m == M - 2)

        def before_last(h):
            o, n, s, e = M * HJ * h, (M - 1) * HJ, HJ * h, HJ * h + HJ
            ft, fd = ps(6 + h, 128, 128 + HJ), ps(6 + h, 256, 256 + HJ)
            tt(ft, ps(6 + h, 0, HJ), A("i_u2", s, e), Op.mult)
            tt(A("f_r", s, e), ft, A("i_r1", s, e), Op.add)
            tt(fd, K("PW1", s, e), A("f_r", s, e), Op.subtract)
            tt(A("f_e", s, e), fd, A("RG", o + M - 2, o + n, M - 1), Op.mult)

        def succ(h):
            s, e = HJ * h, HJ * h + HJ
            ft = ps(6 + h, 128, 128 + HJ)
            ts(ft, ps(h, 0, HJ), K("T", 0, 1), Op.is_ge)
            tt(A("f_d", s, e), ft, A("f_e", s, e), Op.mult)
            tt(A("i_r2", s, e), A("f_r", s, e), A("f_d", s, e), Op.add)
            ts(A("i_nxw", s, e), A("i_r2", s, e), W - 1, Op.bitwise_and)
            cp(A("NXH", s, e), A("i_nxw", s, e))
            for i in range(16):
                mm(ps(WB[h][i // 8], HJ * (i % 8), HJ * (i % 8) + HJ), A("BIh", 128 * i, 128 * i + 128), A("NXH", s, e), True, True)

        def window(h):
            act(A("NXW", H * h, H * h + 512), ps(WB[h][0], 0, 512))
            cp(A("NXW", H * h + 512, H * h + H), ps(WB[h][1], 0, 512))

        calls = {"sg": sgath, "sl": slook, "v": vlook, "a": size, "first": first, "bl": before_last, "succ": succ,
                 "win": window, "lists": lambda: lists(1), "consts": consts_c if r == 0 else (lambda: None)}
        lists(0)
        for step in PLAN:
            calls[step[0]](*step[1:])
        if r == 0:
            consts_b()

        mm(ps(7, 15, 128, 16), K("IDh"), K("ONh"), True, True)
        mm(ps(3, 0, 128, 16), K("IDh"), K("L0h"), True, True)
        prev, last = K("L0"), K("L0h")
        sgather(A("Xk", 0, 128), A(X, 0, W), prev)
        for k in range(1, L):
            o = 128 * (k % 2)
            vgather(A("CM", o, o + 128), A("NXW"), prev, K("MK"), Op.mult)
            scan(A("CS", o, o + 128), K("RSh"), A("CM", o, o + 128), Op.mult, Op.add)
            prev = A("LC", 8 * k, 8 * k + 8)
            now = A("CS", o + 15, o + 128, 16)
            cp(prev, now)
            mm(ps(3, k, 128, 16), K("IDh"), now, True, True)
            mm(ps(7, k - 1, 128, 16), K("NIh"), last, True, False)
            mm(ps(7, k - 1, 128, 16), K("IDh"), now, False, True)
            last = now
            if k == L - 1:
                cp(A("LF"), ps(3, 0, 128))
                act(A("SW"), ps(7, 0, 128), Fn.Abs, bias=1023.0)
            sgather(A("Xk", 128 * k, 128 * k + 128), A(X, 0, W), prev)
        sgather(A("Xst"), A(X, 0, W), A("LF"))

        ts(A("J"), A("SW"), 1024.0, Op.not_equal)
        mm(ps(2, 0, 2 * ND), K("IDN"), K("ZR", 0, 2 * ND), True, False)
        scan(A("INC"), K("ONF"), A("J"), Op.mult, Op.add)
        mm(ps(6, 0, 1), K("LST1"), A("INC", 127, 128), True, True)
        ts(A("ING"), A("INC"), ps(6, 0, 1), Op.add, 200.0, Op.min)
        mm(ps(7, 0, 128), K("DSH"), A("ING"), True, True)
        ts(A("GO"), K("NARR"), ps(6, 0, 1), Op.is_gt)
        cp(A("DEL"), ps(7, 0, 128))
        for c in range(2):
            mm(ps(c, 0, 320), A("DEL"), A("GO", 320 * c, 320 * c + 320), True, True)
        for c in range(2):
            tt(A("CC", 320 * c, 320 * c + 320), ps(c, 0, 320), K("NP1", 320 * c, 320 * c + 320), Op.is_lt)
        for s, w in (("GO", "GW"), ("CC", "CW")):
            for d in range(ND):
                mm(ps(2, 2 * d, 2 * d + 2), A(s, 128 * d, 128 * d + 128), K(w, 0, 2), False, s == "CC" and d == ND - 1)
        ts(A("AL", 0, ND), ps(2, 0, 2 * ND, 2), -1.0, Op.add)
        ak, qn = "ASK%d" % r, "QIN%d" % r
        vgather(A(ak), A("Xk"), A("AL", 0, ND))
        qs = [(Q * d, Q * d + Q) for d in range(ND)]
        landed["q%d" % r] = send([A(ak, *x) for x in qs], [A(qn, *x) for x in qs], [cores[(rank + 1 + d) % N] for d in range(ND)], "q%d" % r, ND - 1)
        ts(A("plc", 0, ND), ps(2, 1, 2 * ND, 2), -128.0, Op.add)
        ts(A("live", 0, ND), A("plc", 0, ND), float(W), Op.is_lt)
        ts(A("pl8", 0, ND), A("plc", 0, ND), 8193.0, Op.add)
        mm(ps(6, 0, 128), K("ID16"), K("JJ"), True, False)
        mm(ps(6, 0, 128), K("IDN"), K("ICOL"), False, False)

        note([], [A(qn)], "q%d" % r, landed["q%d" % r])
        mm(ps(3, 0, 80), A("WBLK"), A(qn), True, True)
        act(A("QREP", 0, 80), A(qn))
        act(A("QREP", 80, 160), A(qn))
        act(A("QREP", 160, 320), A("QREP", 0, 160))
        act(A("QREP", 320, 640), A("QREP", 0, 320))
        act(A("QREP", 640, 960), A("QREP", 0, 320))
        tt(A("VM"), ps(3, 0, 80), K("MK", 0, 80), Op.mult)
        scan(A("VS"), K("RS", 0, 80), A("VM"), Op.mult, Op.add)
        q = lambda n: A("q_" + n, 0, ND)
        cp(q("vi"), A("VS", 15, 80, 16))
        ts(q("va"), q("vi"), W - 1, Op.bitwise_and)
        ts(q("vs"), q("vi"), W - 1, Op.bitwise_and, 5, Op.arith_shift_right)
        ts(q("v2"), q("va"), 2, Op.mult)
        tt(q("vb"), q("va"), q("vs"), Op.mult)
        tt(q("c0"), q("vb"), q("va"), Op.add)
        for d in range(ND):
            ts(A("qraw", d, P * ND, ND), K("MC"), A("q_v2", d, d + 1), Op.mult, A("q_c0", d, d + 1), Op.add)
        ts(A("qmsk"), A("qraw"), W - 1, Op.bitwise_and)
        cp(A("qlst"), A("qmsk"))
        parts = [(0, 60), (60, 120), (120, 160)]
        gb = gslot(640)
        sgather(gb, A(X, 0, W), A("qlst", 120, 160))
        for c in range(2):
            mm(ps(1 - c, 0, 320), K("IDN"), A("G", gb[1] + 320 * c, gb[1] + 320 * c + 320), True, False)
            mm(ps(1 - c, 0, 320), K("NEGI"), A("QREP", 0, 320), False, True)
        for t in (0, 2, 1):
            l0, l1 = parts[t]
            n = 16 * (l1 - l0)
            d, a, o = slot()
            if t < 2:
                vgather(A("D", o, o + n), A(X, 0, W), A("qlst", l0, l1), A("QREP", 0, n), Op.subtract)
                act(A("AB", o, o + n), A("D", o, o + n), Fn.Abs)
            else:
                for c in range(2):
                    act(A("AB", o + 320 * c, o + 320 * c + 320), ps(1 - c, 0, 320), Fn.Abs)
            mm(ps(4, l0, l1), K("IDN"), K("MROW", l0, l1), True, False)
            for i in range(16):
                mm(ps(4, l0, l1), A("EI", 128 * i, 128 * i + 128), A("AB", o + i, o + n, 16), False, i == 15)
        for d in range(ND):
            a, b = A("q_KM", d, d + 1), ps(4, d, P * ND, ND)
            do("V", lambda: g.vector.tensor_reduce(ap(a), ap(b), AxisListType.X, Op.min), [b], [a])
        ts(q("ki"), q("KM"), float(P), Op.mult)
        fl = "FIL%d" % r
        ts(q("km"), q("ki"), P - 1, Op.bitwise_and)
        tt(q("kt"), q("km"), q("v2"), Op.mult)
        tt(q("kc"), q("kt"), q("c0"), Op.add)
        ts(q("kd"), q("kc"), W - 1, Op.bitwise_and)
        for f in range(F):
            ts(A("FL", f, F * ND, F), q("kd"), f + 1, Op.add)
        ts(A(fl, Q * F, ND * SLOT, SLOT), q("KM"), K("T", 1, 2), Op.is_lt)
        for d in (0, 3, 1, 4, 2):
            (sgather if d > 2 else vgather)(A(fl, SLOT * d, SLOT * d + Q * F), A(X, 0, W + 8), A("FL", F * d, F * d + F))
        z = "ZIN%d" % r
        zs = [(SLOT * d, SLOT * d + SLOT) for d in range(ND)]
        landed["z%d" % r] = send([A(fl, *x) for x in zs], [A(z, *x) for x in zs], [cores[(rank - 1 - d) % N] for d in range(ND)], "z%d" % r, 2)
        for i in range(16):
            act(A("Xnat", 128 * i, 128 * i + 128), A("Xst", i, W, 16))

        note([], [A(z)], "z%d" % r, landed["z%d" % r])
        tt(A("an", 0, ND), A(z, Q * F, ND * SLOT, SLOT), A("live", 0, ND), Op.mult)
        mm(ps(5, 0, ND), K("LST6"), A("an", 0, ND), True, False)
        for k in range(1, ND):
            mm(ps(5, k, ND), K("BLK6"), A("an", 0, ND - k), False, False)
        mm(ps(5, 0, ND), K("N8I"), A("an", 0, ND), False, True)
        tt(A("a8", 0, ND), ps(5, 0, ND), A("pl8", 0, ND), Op.add)
        ts(A("ahl", 0, ND), A("a8", 0, ND), 4, Op.arith_shift_right)
        ts(A("ahl", ND, 2 * ND), A("a8", 0, ND), 15, Op.bitwise_and)
        cp(A("ahf", 0, 2 * ND), A("ahl", 0, 2 * ND))
        for d in range(ND):
            o = 128 * d
            hi, lo = A("ahf", d, d + 1), A("ahf", ND + d, ND + d + 1)
            ts(A("LT", o, o + 128), K("JJ"), hi, Op.is_gt)
            ts(A("EQ", o, o + 128), K("JJ"), hi, Op.is_equal)
            ts(A("LO", o, o + 128), K("IARR"), lo, Op.is_gt, -6.0, Op.mult)
            mm(ps(6, 0, 128), K("NB6"), A("LT", o, o + 128), False, False)
            mm(ps(6, 0, 128), A("LO", o, o + 128), A("EQ", o, o + 128), False, d == ND - 1)
        for f in range(F):
            ts(A("SL", f, F * ND, F), A("a8", 0, ND), f, Op.add)
        tt(A("SL2", 0, 30), A("SL", 0, 30), K("JK", 0, 30), Op.min)
        cp(A("SLu", 0, 30), A("SL2", 0, 30))
        ts(A("PL", HJ, 2 * HJ), ps(6, HJ, 2 * HJ), 0.0, Op.max)
        ts(A("PL", 0, HJ), ps(6, 0, HJ), 0.0, Op.max)
        sgather(A(XN, H, W), A("Xnat"), A("PL", HJ, 2 * HJ))
        vgather(A(XN, 0, H), A("Xnat"), A("PL", 0, HJ))
        for d in range(ND):
            scatter(A(XN), A("SLu", F * d, F * d + F), A(z, SLOT * d, SLOT * d + Q * F))
        if r + 1 < RO:
            act(A(XN, W, W + 8), A(XN, 0, 8))

    dma("Y", T.y[:, 0:H], T.XC[:, 0:H], "dy0", [A("XC", 0, H)], [])
    dma("S", T.y[:, H:W], T.XC[:, H:W], "dy1", [A("XC", H, W)], [])
    for e in ("V", "S", "T", "G"):
        wait("G", semof[e], cnt[e])
    g.wait_ge(T.sem.lsem, tot[0])
    for s in ("dwt", "dx0", "dx1", "dth", "dy0", "dy1"):
        g.wait_ge(T.sem[s], 16)
    for s in ("q0", "q1", "z0", "z1"):
        g.wait_ge(T.sem[s], landed[s])
